import numpy as np
import ml_dtypes


def mxq(x, axis, fmt="e4m3"):
    dtype, down = {"e4m3": (ml_dtypes.float8_e4m3fn, 7), "e5m2": (ml_dtypes.float8_e5m2, 14)}[fmt]
    v = np.moveaxis(np.asarray(x, np.float32).astype(ml_dtypes.bfloat16).astype(np.float64), axis, -1)
    blocks = v.reshape(v.shape[:-1] + (-1, 32))
    amax = np.abs(blocks).max(-1, keepdims=True)
    byte = np.maximum(np.where(amax > 0, np.frexp(amax)[1] - 1 + 127, 0) - down, 1)
    scale = np.exp2(byte - 127.0)
    codes = (blocks / scale).astype(np.float32).astype(dtype).astype(np.float64)
    return np.moveaxis((codes * scale).reshape(v.shape), -1, axis)


WIDE = False


def mx_kscale(k):
    if not WIDE:
        return np.ones(k)
    levels = np.array([10, -10, 5, -5, 0])
    if k % 512:
        return np.exp2(np.random.permutation(np.resize(levels, k // 32))).repeat(32)
    a = np.empty((k // 512, 16))
    for p in range(k // 512):
        a[p, :8] = np.random.permutation(np.resize(levels, 8))
        for g in range(8):
            far = levels[np.abs(levels - a[p, g]) >= 10]
            a[p, g + 8] = far[np.random.randint(len(far))]
    return np.exp2(a.ravel()).repeat(32)


def f64(x):
    return np.asarray(x).astype(np.float64)


def striped(idx):
    return np.tile(idx.reshape(-1, 16).T, (8, 1)).astype(np.uint16)


def unstriped(offs):
    return offs[:16].T.reshape(-1).astype(np.int64)


def pack_weight(w):
    k, n = w.shape
    w = f64(np.asarray(w, np.float32).astype(ml_dtypes.bfloat16)).reshape(k // 32, 32, n)
    amax = np.abs(w).max(1)
    byte = np.clip(np.where(amax > 0, np.frexp(amax)[1] - 1 + 127 - 7, 1), 1, 254)
    scaled = (w * np.exp2(127.0 - byte)[:, None, :]).reshape(k, n).astype(np.float32)
    words = np.ascontiguousarray(scaled.reshape(k // 512, 128, 4, n).transpose(0, 1, 3, 2)).astype(ml_dtypes.float8_e4m3fn).view(np.uint8)
    return words, np.ascontiguousarray(byte.astype(np.uint8).reshape(k // 512, 16, n))


def unpack_weight(words, scales):
    g, p, n, _ = words.shape
    vals = np.ascontiguousarray(words).view(ml_dtypes.float8_e4m3fn).astype(np.float64) * np.repeat(np.exp2(scales.astype(np.float64) - 127.0), 8, axis=1)[..., None]
    return vals.transpose(0, 1, 3, 2).reshape(g * 512, n)


def planes(y):
    n, m = y.shape
    v = y.astype(np.float32).astype(ml_dtypes.bfloat16).astype(np.float64).reshape(n // 32, 32, m)
    top = np.abs(v).max(1)
    byte = np.clip(np.where(top > 0, np.frexp(top)[1] - 1 + 127 - 7, 1), 1, 254)
    codes = (v * np.exp2(127.0 - byte)[:, None, :]).reshape(n, m).astype(np.float32).astype(ml_dtypes.float8_e4m3fn).view(np.uint8)
    words = codes.reshape(n // 512, 128, 4, m).transpose(0, 1, 3, 2)
    return np.ascontiguousarray(words), np.ascontiguousarray(byte.astype(np.uint8).reshape(n // 512, 16, m))


K, T, S, D, V, H = 512, 2048, 512, 2, 256, 512
P = 2 ** 7


def setup_inputs():
    n = np.random.standard_normal
    s = mx_kscale(K)[:, None]
    u = mx_kscale(H)
    near = np.random.permutation(S)
    packed_xT = pack_weight(n((K, T)) * s)
    packed_w2 = pack_weight(n((H, H)) / np.sqrt(H) / u[:, None])
    return {
        "x_words": packed_xT[0],
        "x_scales": packed_xT[1],
        "w1": (n((K, H)) / np.sqrt(K) / s * u).astype(np.float32),
        "w2_words": packed_w2[0],
        "w2_scales": packed_w2[1],
        "gate": (np.tile(np.random.uniform(0.2, 1.0, (D, 1, V)) / np.sqrt(D), (1, P, 1))).astype(np.float32),
        "turn": (np.random.uniform(0.5, 1.5, (H, 1)) * u[:, None]).astype(np.float32),
        "offs": striped(np.random.permutation(T)[:S]),
        "cen": striped(np.random.permutation(S)[:V]),
        "pos1": striped(near[:V]),
        "pos2": striped(near[V:]),
    }


def reference(x_words, x_scales, w1, w2_words, w2_scales, gate, turn, offs, cen, pos1, pos2):
    xq = unpack_weight(x_words, x_scales)[:, unstriped(offs)]
    h = mxq(f64(w1), 0, "e4m3").T @ xq
    z = 0.9 * (h[:, unstriped(pos1)] * f64(gate)[0, :1] + h[:, unstriped(pos2)] * f64(gate)[1, :1]) + 0.1 * h[:, unstriped(cen)]
    y = unpack_weight(w2_words, w2_scales).T @ mxq(z, 0, "e4m3")
    out_0 = 0.6 * z + 0.4 * (f64(turn) * y)
    return (out_0,) + planes(out_0)

@@ -1,0 +1,164 @@
+from contextlib import ExitStack
+
+import concourse.mybir as mybir
+
+K, T, S, V, H = 512, 2048, 512, 256, 512
+P = 128
+PACK = 4
+HALF = V // 2
+FLOPS = 2 * K * H * S + 2 * H * H * V
+
+F32 = mybir.dt.float32
+BF16 = mybir.dt.bfloat16
+I32 = mybir.dt.int32
+U32 = mybir.dt.uint32
+U16 = mybir.dt.uint16
+U8 = mybir.dt.uint8
+FP8X4 = mybir.dt.float8_e4m3fn_x4
+MULT = mybir.AluOpType.mult
+ADD = mybir.AluOpType.add
+COPY = mybir.ActivationFunctionType.Copy
+
+
+def tile_picked_zgcnii_none_po_kernel(
+    tc, x_words, x_scales, w1, w2_words, w2_scales, gate, turn, offs, cen, pos1, pos2, out_0, out_1, out_2
+):
+    nc = tc.nc
+    with ExitStack() as ctx:
+        keep = ctx.enter_context(tc.tile_pool(name="keep", bufs=1))
+        shared = ctx.enter_context(tc.tile_pool(name="shared", bufs=1))
+        psum = ctx.enter_context(tc.psum_pool(name="psum", bufs=1))
+
+        offs_sb = keep.tile([P, S // 16], U16, name="offs_sb")
+        cen_sb = keep.tile([P, V // 16], U16, name="cen_sb")
+        pos1_sb = keep.tile([P, V // 16], U16, name="pos1_sb")
+        pos2_sb = keep.tile([P, V // 16], U16, name="pos2_sb")
+        xs_all = shared.tile([P, T], U8, name="xs_all", align_bytes=64, offset=0)
+        xw_all = shared.tile([P, T], I32, name="xw_all", align_bytes=64, offset=2048)
+        w1_raw = shared.tile([P, PACK, H], F32, name="w1_raw", align_bytes=64, offset=10240)
+        turn_raw = keep.tile([P, PACK], F32, name="turn_raw", align_bytes=64)
+
+        nc.vector.memset(xs_all[:].bitcast(I32), 0)
+        nc.sync.dma_start(offs_sb[:], offs)
+        nc.sync.dma_start(pos1_sb[:], pos1)
+        nc.sync.dma_start(w1_raw[:], w1.rearrange("(p j) c -> p j c", j=PACK))
+        nc.sync.dma_start(pos2_sb[:], pos2)
+        nc.sync.dma_start(cen_sb[:], cen)
+        nc.sync.dma_start(xw_all[:], x_words[0].rearrange("p n t -> p (n t)").bitcast(I32))
+        for q in range(4):
+            nc.scalar.dma_start(xs_all[32 * q : 32 * q + 4, :].bitcast(I32), x_scales[0, 4 * q : 4 * q + 4, :].bitcast(I32))
+        nc.gpsimd.dma_start(turn_raw[:], turn.rearrange("(p t) o -> p (t o)", t=PACK))
+
+        turn_sc = keep.tile([P, PACK], F32, name="turn_sc", align_bytes=64)
+        nc.scalar.activation(turn_sc[:], turn_raw[:], COPY, scale=0.4)
+
+        xq_scales = keep.tile([P, S], U8, name="xq_scales", align_bytes=64)
+        nc.vector.tensor_copy(xq_scales[:], xs_all[:].indirect(offs_sb[:]))
+
+        w1_bf = keep.tile([P, PACK, P, PACK], BF16, name="w1_bf", align_bytes=64)
+        src = w1_raw[:].rearrange("p j (m t) -> p m t j", t=PACK)
+        dst = w1_bf[:].rearrange("p t m j -> p m t j")
+        split = 72
+        nc.vector.tensor_copy(dst[:, :split], src[:, :split])
+        nc.scalar.copy(dst[:, split:], src[:, split:])
+        gate_raw = shared.tile([P, 2, V], F32, name="gate_raw", align_bytes=64, offset=14336)
+        nc.sync.dma_start(gate_raw[:], gate.rearrange("d p v -> p d v"))
+        w2w_raw = shared.tile([P, H], I32, name="w2w_raw", align_bytes=64, offset=10240)
+        nc.sync.dma_start(w2w_raw[:], w2_words[0].rearrange("p n t -> p (n t)").bitcast(I32))
+        w2s_raw = shared.tile([P, H], U8, name="w2s_raw", align_bytes=64, offset=12288)
+        nc.vector.memset(w2s_raw[:].bitcast(I32), 0)
+        for q in range(4):
+            nc.sync.dma_start(w2s_raw[32 * q : 32 * q + 4, :].bitcast(I32), w2_scales[0, 4 * q : 4 * q + 4, :].bitcast(I32))
+        w1_words = keep.tile([P, H], U32, name="w1_words", align_bytes=64)
+        w1_scales = keep.tile([P, H], U8, name="w1_scales", align_bytes=64)
+        nc.vector.quantize_mx(out=w1_words[:].bitcast(FP8X4), scales=w1_scales[:], in_=w1_bf[:].rearrange("p t m j -> p (t m j)"))
+
+        xq_words = [keep.tile([P, S // 2], U32, name="xq_words%d" % c, align_bytes=64) for c in range(2)]
+        for c in range(2):
+            nc.vector.tensor_copy(xq_words[c][:], xw_all[:].bitcast(U32).indirect(offs_sb[:, 16 * c : 16 * (c + 1)]))
+
+        h = [keep.tile([P, S], F32, name="h%d" % t, align_bytes=64) for t in range(PACK)]
+        for t in range(PACK):
+            rows = slice(P * t, P * (t + 1))
+            for c in range(2):
+                cols = slice(256 * c, 256 * (c + 1))
+                bank = psum.tile([P, 512], F32, name="bank", tag="bank%d" % (2 * t + c))
+                nc.tensor.matmul_mx(
+                    out=bank[:, :256], lhsT=w1_words[:, rows].bitcast(FP8X4), lhsT_scale=w1_scales[:, rows],
+                    rhs=xq_words[c][:].bitcast(FP8X4), rhs_scale=xq_scales[:, cols], start=True, stop=True,
+                )
+                nc.scalar.activation(h[t][:, cols], bank[:, :256], COPY, scale=0.06)
+
+        gate_sc = [shared.tile([P, V], F32, name="gate_sc%d" % d, align_bytes=64, offset=2048 + 1024 * d) for d in range(2)]
+        for d in range(2):
+            nc.vector.tensor_scalar_mul(gate_sc[d][:], gate_raw[:, d, :], 9.0)
+
+        w2w = shared.tile([P, H], U32, name="w2w", align_bytes=64, offset=4096)
+        w2s = shared.tile([P, H], U8, name="w2s", align_bytes=64, offset=6144)
+        nc.vector.tensor_copy(
+            w2w[:].rearrange("p (t a b) -> p a t b", t=PACK, b=4),
+            w2w_raw[:].bitcast(U32).rearrange("p (a b t) -> p a t b", t=PACK, b=4),
+        )
+        nc.vector.tensor_copy(w2s[:].rearrange("p (t m) -> p m t", t=PACK), w2s_raw[:].rearrange("p (m t) -> p m t", t=PACK))
+
+        first = keep.tile([P, PACK, V], F32, name="first", align_bytes=64)
+        second = keep.tile([P, PACK, V], F32, name="second", align_bytes=64)
+        for t in range(PACK):
+            nc.vector.tensor_tensor(first[:, t, :], h[t][:].indirect(pos1_sb[:]), gate_sc[0][:], MULT)
+            nc.vector.tensor_tensor(second[:, t, :], h[t][:].indirect(pos2_sb[:]), gate_sc[1][:], MULT)
+        both = [
+            shared.tile([P, 2, V], F32, name="both0", align_bytes=64, offset=1024),
+            keep.tile([P, 2, V], F32, name="both1", align_bytes=64),
+        ]
+        for u in range(2):
+            nc.vector.tensor_tensor(both[u][:], first[:, 2 * u : 2 * u + 2, :], second[:, 2 * u : 2 * u + 2, :], ADD)
+
+        o_words = keep.tile([P, V], I32, name="o_words", align_bytes=64)
+        o_scales = keep.tile([P, V], U8, name="o_scales", align_bytes=64)
+        out_rows = out_0.rearrange("(p t) v -> p t v", t=PACK)
+        out_words = out_1[0].rearrange("p n t -> p (n t)").bitcast(I32)
+        zs = [keep.tile([P, PACK, HALF], F32, name="zs%d" % a, align_bytes=64) for a in range(2)]
+        for a in range(2):
+            cols = slice(HALF * a, HALF * (a + 1))
+            lst = slice(HALF // 16 * a, HALF // 16 * (a + 1))
+            for t in range(PACK):
+                nc.vector.tensor_tensor(zs[a][:, t, :], h[t][:].indirect(cen_sb[:, lst]), both[t // 2][:, t % 2, cols], ADD)
+        banks = {}
+        for a in range(2):
+            z_bf = keep.tile([P, HALF, PACK], BF16, name="z_bf%d" % a, align_bytes=64)
+            woven = z_bf[:].rearrange("p (c i) t -> p c t i", i=4)
+            planes = zs[a][:].rearrange("p t (c i) -> p c t i", i=4)
+            if a == 0:
+                nc.scalar.activation(woven, planes, COPY, scale=1.0 / 0.6)
+            else:
+                nc.vector.tensor_scalar_mul(woven, planes, 1.0 / 0.6)
+            z_words = keep.tile([P, HALF], U32, name="z_words%d" % a, align_bytes=64)
+            z_scales = keep.tile([P, HALF], U8, name="z_scales%d" % a, align_bytes=64)
+            nc.vector.quantize_mx(out=z_words[:].bitcast(FP8X4), scales=z_scales[:], in_=z_bf[:].rearrange("p c t -> p (c t)"))
+            for t in range(PACK):
+                rows = slice(P * t, P * (t + 1))
+                banks[a, t] = psum.tile([P, 512], F32, name="bank", tag="bank%d" % (PACK * a + t))
+                nc.tensor.matmul_mx(
+                    out=banks[a, t][:, :HALF], lhsT=w2w[:, rows].bitcast(FP8X4), lhsT_scale=w2s[:, rows],
+                    rhs=z_words[:].bitcast(FP8X4), rhs_scale=z_scales[:], start=True, stop=True,
+                )
+        for a in range(2):
+            cols = slice(HALF * a, HALF * (a + 1))
+            res = keep.tile([P, PACK, HALF], F32, name="res%d" % a, align_bytes=64)
+            for t in range(PACK):
+                nc.vector.scalar_tensor_tensor(res[:, t, :], banks[a, t][:, :HALF], turn_sc[:, t : t + 1], zs[a][:, t, :], MULT, ADD)
+            nc.sync.dma_start(out_rows[:, :, cols], res[:])
+            res_bf = keep.tile([P, HALF, PACK], BF16, name="res_bf%d" % a, align_bytes=64)
+            woven = res_bf[:].rearrange("p (c i) t -> p c t i", i=4)
+            planes = res[:].rearrange("p t (c i) -> p c t i", i=4)
+            if a == 0:
+                nc.scalar.copy(woven, planes)
+            else:
+                nc.vector.tensor_copy(woven, planes)
+            nc.vector.quantize_mx(
+                out=o_words[:, cols].bitcast(FP8X4), scales=o_scales[:, cols], in_=res_bf[:].rearrange("p c t -> p (c t)")
+            )
+            nc.sync.dma_start(out_words[:, cols], o_words[:, cols])
+        for q in range(4):
+            eng = nc.sync if q % 2 == 0 else nc.scalar
+            eng.dma_start(out_2[0, 4 * q : 4 * q + 4, :].bitcast(I32), o_scales[32 * q : 32 * q + 4, :].bitcast(I32))

@@ -35,45 +35,52 @@ def tile_picked_zgcnii_none_po_kernel(
         pos2_sb = keep.tile([P, V // 16], U16, name="pos2_sb")
         xs_all = shared.tile([P, T], U8, name="xs_all", align_bytes=64, offset=0)
         xw_all = shared.tile([P, T], I32, name="xw_all", align_bytes=64, offset=2048)
-        w1_raw = shared.tile([P, PACK, H], F32, name="w1_raw", align_bytes=64, offset=10240)
+        w1_raw = [shared.tile([P, PACK, H // 2], F32, name="w1_raw%d" % c, align_bytes=64, offset=10240 + 4096 * c) for c in range(2)]
+        w2s_raw = keep.tile([P, H], U8, name="w2s_raw", align_bytes=64)
         turn_raw = keep.tile([P, PACK], F32, name="turn_raw", align_bytes=64)
 
         nc.vector.memset(xs_all[:].bitcast(I32), 0)
+        nc.gpsimd.memset(w2s_raw[:].bitcast(I32), 0)
+        w1_rows = w1.rearrange("(p j) c -> p j c", j=PACK)
         nc.sync.dma_start(offs_sb[:], offs)
         nc.sync.dma_start(pos1_sb[:], pos1)
-        nc.sync.dma_start(w1_raw[:], w1.rearrange("(p j) c -> p j c", j=PACK))
+        nc.sync.dma_start(w1_raw[0][:], w1_rows[:, :, : H // 2])
         nc.sync.dma_start(pos2_sb[:], pos2)
+        nc.sync.dma_start(w1_raw[1][:], w1_rows[:, :, H // 2 :])
         nc.sync.dma_start(cen_sb[:], cen)
         nc.sync.dma_start(xw_all[:], x_words[0].rearrange("p n t -> p (n t)").bitcast(I32))
         for q in range(4):
             nc.scalar.dma_start(xs_all[32 * q : 32 * q + 4, :].bitcast(I32), x_scales[0, 4 * q : 4 * q + 4, :].bitcast(I32))
         nc.gpsimd.dma_start(turn_raw[:], turn.rearrange("(p t) o -> p (t o)", t=PACK))
+        for q in range(4):
+            nc.gpsimd.dma_start(w2s_raw[32 * q : 32 * q + 4, :].bitcast(I32), w2_scales[0, 4 * q : 4 * q + 4, :].bitcast(I32))
 
         turn_sc = keep.tile([P, PACK], F32, name="turn_sc", align_bytes=64)
-        nc.scalar.activation(turn_sc[:], turn_raw[:], COPY, scale=0.4)
+        nc.gpsimd.tensor_scalar(turn_sc[:], turn_raw[:], 0.4, 0.0, MULT, ADD)
 
         xq_scales = keep.tile([P, S], U8, name="xq_scales", align_bytes=64)
         nc.vector.tensor_copy(xq_scales[:], xs_all[:].indirect(offs_sb[:]))
 
-        w1_bf = keep.tile([P, PACK, P, PACK], BF16, name="w1_bf", align_bytes=64)
-        src = w1_raw[:].rearrange("p j (m t) -> p m t j", t=PACK)
-        dst = w1_bf[:].rearrange("p t m j -> p m t j")
-        split = 72
-        nc.vector.tensor_copy(dst[:, :split], src[:, :split])
-        nc.scalar.copy(dst[:, split:], src[:, split:])
-        gate_raw = shared.tile([P, 2, V], F32, name="gate_raw", align_bytes=64, offset=14336)
-        nc.sync.dma_start(gate_raw[:], gate.rearrange("d p v -> p d v"))
-        w2w_raw = shared.tile([P, H], I32, name="w2w_raw", align_bytes=64, offset=10240)
-        nc.sync.dma_start(w2w_raw[:], w2_words[0].rearrange("p n t -> p (n t)").bitcast(I32))
-        w2s_raw = shared.tile([P, H], U8, name="w2s_raw", align_bytes=64, offset=12288)
-        nc.vector.memset(w2s_raw[:].bitcast(I32), 0)
-        for q in range(4):
-            nc.sync.dma_start(w2s_raw[32 * q : 32 * q + 4, :].bitcast(I32), w2_scales[0, 4 * q : 4 * q + 4, :].bitcast(I32))
         w1_words = keep.tile([P, H], U32, name="w1_words", align_bytes=64)
         w1_scales = keep.tile([P, H], U8, name="w1_scales", align_bytes=64)
-        nc.vector.quantize_mx(out=w1_words[:].bitcast(FP8X4), scales=w1_scales[:], in_=w1_bf[:].rearrange("p t m j -> p (t m j)"))
+        split = 40
+        for c in range(2):
+            w1_bf = keep.tile([P, PACK, P // 2, PACK], BF16, name="w1_bf%d" % c, align_bytes=64)
+            src = w1_raw[c][:].rearrange("p j (m t) -> p m t j", t=PACK)
+            dst = w1_bf[:].rearrange("p t m j -> p m t j")
+            nc.vector.tensor_copy(dst[:, :split], src[:, :split])
+            nc.scalar.copy(dst[:, split:], src[:, split:])
+            for t in range(PACK):
+                cols = slice(P * t + 64 * c, P * t + 64 * (c + 1))
+                nc.vector.quantize_mx(
+                    out=w1_words[:, cols].bitcast(FP8X4), scales=w1_scales[:, cols], in_=w1_bf[:, t].rearrange("p m j -> p (m j)")
+                )
+        gate_raw = shared.tile([P, 2, V], F32, name="gate_raw", align_bytes=64, offset=10240)
+        nc.sync.dma_start(gate_raw[:], gate.rearrange("d p v -> p d v"))
+        w2w_raw = shared.tile([P, H], I32, name="w2w_raw", align_bytes=64, offset=12288)
+        nc.sync.dma_start(w2w_raw[:], w2_words[0].rearrange("p n t -> p (n t)").bitcast(I32))
 
-        xq_words = [keep.tile([P, S // 2], U32, name="xq_words%d" % c, align_bytes=64) for c in range(2)]
+        xq_words = [shared.tile([P, S // 2], U32, name="xq_words%d" % c, align_bytes=64, offset=1024 * c) for c in range(2)]
         for c in range(2):
             nc.vector.tensor_copy(xq_words[c][:], xw_all[:].bitcast(U32).indirect(offs_sb[:, 16 * c : 16 * (c + 1)]))
 
@@ -99,7 +106,10 @@ def tile_picked_zgcnii_none_po_kernel(
             w2w[:].rearrange("p (t a b) -> p a t b", t=PACK, b=4),
             w2w_raw[:].bitcast(U32).rearrange("p (a b t) -> p a t b", t=PACK, b=4),
         )
-        nc.vector.tensor_copy(w2s[:].rearrange("p (t m) -> p m t", t=PACK), w2s_raw[:].rearrange("p (m t) -> p m t", t=PACK))
+        nc.vector.tensor_copy(
+            w2s[:].rearrange("p (t a b) -> p a t b", t=PACK, b=16),
+            w2s_raw[:].rearrange("p (a b t) -> p a t b", t=PACK, b=16),
+        )
 
         first = keep.tile([P, PACK, V], F32, name="first", align_bytes=64)
         second = keep.tile([P, PACK, V], F32, name="second", align_bytes=64)

@@ -1,6 +1,7 @@
 from contextlib import ExitStack
 
 import concourse.mybir as mybir
+from concourse.masks import make_identity
 
 K, T, S, V, H = 512, 2048, 512, 256, 512
 P = 128
@@ -44,8 +45,8 @@ def tile_picked_zgcnii_none_po_kernel(
         w1_rows = w1.rearrange("(p j) c -> p j c", j=PACK)
         nc.sync.dma_start(offs_sb[:], offs)
         nc.sync.dma_start(pos1_sb[:], pos1)
-        nc.sync.dma_start(w1_raw[0][:], w1_rows[:, :, : H // 2])
         nc.sync.dma_start(pos2_sb[:], pos2)
+        nc.sync.dma_start(w1_raw[0][:], w1_rows[:, :, : H // 2])
         nc.sync.dma_start(w1_raw[1][:], w1_rows[:, :, H // 2 :])
         nc.sync.dma_start(cen_sb[:], cen)
         nc.sync.dma_start(xw_all[:], x_words[0].rearrange("p n t -> p (n t)").bitcast(I32))
@@ -54,6 +55,8 @@ def tile_picked_zgcnii_none_po_kernel(
         nc.gpsimd.dma_start(turn_raw[:], turn.rearrange("(p t) o -> p (t o)", t=PACK))
         for q in range(4):
             nc.gpsimd.dma_start(w2s_raw[32 * q : 32 * q + 4, :].bitcast(I32), w2_scales[0, 4 * q : 4 * q + 4, :].bitcast(I32))
+        ident = keep.tile([P, P], F32, name="ident", align_bytes=64)
+        make_identity(nc, ident[:])
 
         turn_sc = keep.tile([P, PACK], F32, name="turn_sc", align_bytes=64)
         nc.gpsimd.tensor_scalar(turn_sc[:], turn_raw[:], 0.4, 0.0, MULT, ADD)
@@ -80,32 +83,31 @@ def tile_picked_zgcnii_none_po_kernel(
         w2w_raw = shared.tile([P, H], I32, name="w2w_raw", align_bytes=64, offset=12288)
         nc.sync.dma_start(w2w_raw[:], w2_words[0].rearrange("p n t -> p (n t)").bitcast(I32))
 
-        xq_words = [shared.tile([P, S // 2], U32, name="xq_words%d" % c, align_bytes=64, offset=1024 * c) for c in range(2)]
+        gate_sc = shared.tile([P, 2, V], F32, name="gate_sc", align_bytes=64, offset=14336)
+        nc.scalar.activation(gate_sc[:], gate_raw[:], COPY, scale=9.0)
+
+        xq_words = shared.tile([P, S], U32, name="xq_words", align_bytes=64, offset=0)
         for c in range(2):
-            nc.vector.tensor_copy(xq_words[c][:], xw_all[:].bitcast(U32).indirect(offs_sb[:, 16 * c : 16 * (c + 1)]))
+            nc.vector.tensor_copy(xq_words[:, 256 * c : 256 * (c + 1)], xw_all[:].bitcast(U32).indirect(offs_sb[:, 16 * c : 16 * (c + 1)]))
 
         h = [keep.tile([P, S], F32, name="h%d" % t, align_bytes=64) for t in range(PACK)]
-        for t in range(PACK):
+        pieces = [(0, 0, 256), (0, 256, 384), (0, 384, 512)] + [(t, 0, S) for t in range(1, PACK)]
+        for n, (t, lo, hi) in enumerate(pieces):
             rows = slice(P * t, P * (t + 1))
-            for c in range(2):
-                cols = slice(256 * c, 256 * (c + 1))
-                bank = psum.tile([P, 512], F32, name="bank", tag="bank%d" % (2 * t + c))
-                nc.tensor.matmul_mx(
-                    out=bank[:, :256], lhsT=w1_words[:, rows].bitcast(FP8X4), lhsT_scale=w1_scales[:, rows],
-                    rhs=xq_words[c][:].bitcast(FP8X4), rhs_scale=xq_scales[:, cols], start=True, stop=True,
-                )
-                nc.scalar.activation(h[t][:, cols], bank[:, :256], COPY, scale=0.06)
+            bank = psum.tile([P, 512], F32, name="bank", tag="bank%d" % n)
+            nc.tensor.matmul_mx(
+                out=bank[:, : hi - lo], lhsT=w1_words[:, rows].bitcast(FP8X4), lhsT_scale=w1_scales[:, rows],
+                rhs=xq_words[:, lo:hi].bitcast(FP8X4), rhs_scale=xq_scales[:, lo:hi], start=True, stop=True,
+            )
+            nc.scalar.activation(h[t][:, lo:hi], bank[:, : hi - lo], COPY, scale=0.06)
 
-        gate_sc = [shared.tile([P, V], F32, name="gate_sc%d" % d, align_bytes=64, offset=2048 + 1024 * d) for d in range(2)]
-        for d in range(2):
-            nc.vector.tensor_scalar_mul(gate_sc[d][:], gate_raw[:, d, :], 9.0)
 
         w2w = shared.tile([P, H], U32, name="w2w", align_bytes=64, offset=4096)
-        w2s = shared.tile([P, H], U8, name="w2s", align_bytes=64, offset=6144)
         nc.vector.tensor_copy(
             w2w[:].rearrange("p (t a b) -> p a t b", t=PACK, b=4),
             w2w_raw[:].bitcast(U32).rearrange("p (a b t) -> p a t b", t=PACK, b=4),
         )
+        w2s = shared.tile([P, H], U8, name="w2s", align_bytes=64, offset=6144)
         nc.vector.tensor_copy(
             w2s[:].rearrange("p (t a b) -> p a t b", t=PACK, b=16),
             w2s_raw[:].rearrange("p (a b t) -> p a t b", t=PACK, b=16),
@@ -113,26 +115,43 @@ def tile_picked_zgcnii_none_po_kernel(
 
         first = keep.tile([P, PACK, V], F32, name="first", align_bytes=64)
         second = keep.tile([P, PACK, V], F32, name="second", align_bytes=64)
-        for t in range(PACK):
-            nc.vector.tensor_tensor(first[:, t, :], h[t][:].indirect(pos1_sb[:]), gate_sc[0][:], MULT)
-            nc.vector.tensor_tensor(second[:, t, :], h[t][:].indirect(pos2_sb[:]), gate_sc[1][:], MULT)
         both = [
-            shared.tile([P, 2, V], F32, name="both0", align_bytes=64, offset=1024),
-            keep.tile([P, 2, V], F32, name="both1", align_bytes=64),
+            [
+                shared.tile([P, HALF], F32, name="both%d_0" % t, align_bytes=64, offset=8192 + 512 * t),
+                keep.tile([P, HALF], F32, name="both%d_1" % t, align_bytes=64),
+            ]
+            for t in range(PACK)
         ]
-        for u in range(2):
-            nc.vector.tensor_tensor(both[u][:], first[:, 2 * u : 2 * u + 2, :], second[:, 2 * u : 2 * u + 2, :], ADD)
+        halves = [slice(HALF * a, HALF * (a + 1)) for a in range(2)]
+        for t in range(PACK):
+            nc.vector.tensor_tensor(first[:, t, :], h[t][:].indirect(pos1_sb[:]), gate_sc[:, 0, :], MULT)
+            nc.vector.tensor_tensor(second[:, t, :], h[t][:].indirect(pos2_sb[:]), gate_sc[:, 1, :], MULT)
+            if t < PACK - 1:
+                turn_banks = [psum.tile([P, 512], F32, name="bank", tag="bank%d" % ((2 * t + a + 6) % 8)) for a in range(2)]
+                turned = [keep.tile([P, P], F32, name="turned%d_%d" % (t, a), align_bytes=64) for a in range(2)]
+                for a in range(2):
+                    nc.tensor.matmul(turn_banks[a][:, :P], first[:, t, halves[a]], ident[:], start=True, stop=False, is_transpose=True)
+                    nc.tensor.matmul(turn_banks[a][:, :P], second[:, t, halves[a]], ident[:], start=False, stop=True, is_transpose=True)
+                    nc.scalar.copy(turned[a][:], turn_banks[a][:, :P])
+                for a in range(2):
+                    nc.tensor.transpose(turn_banks[a][:, P : 2 * P], turned[a][:], ident[:])
+                    nc.scalar.copy(both[t][a][:], turn_banks[a][:, P : 2 * P])
 
         o_words = keep.tile([P, V], I32, name="o_words", align_bytes=64)
         o_scales = keep.tile([P, V], U8, name="o_scales", align_bytes=64)
         out_rows = out_0.rearrange("(p t) v -> p t v", t=PACK)
         out_words = out_1[0].rearrange("p n t -> p (n t)").bitcast(I32)
-        zs = [keep.tile([P, PACK, HALF], F32, name="zs%d" % a, align_bytes=64) for a in range(2)]
+        zs = [
+            shared.tile([P, PACK, HALF], F32, name="zs0", align_bytes=64, offset=14336),
+            shared.tile([P, PACK, HALF], F32, name="zs1", align_bytes=64, offset=8192),
+        ]
         for a in range(2):
-            cols = slice(HALF * a, HALF * (a + 1))
             lst = slice(HALF // 16 * a, HALF // 16 * (a + 1))
             for t in range(PACK):
-                nc.vector.tensor_tensor(zs[a][:, t, :], h[t][:].indirect(cen_sb[:, lst]), both[t // 2][:, t % 2, cols], ADD)
+                nc.vector.tensor_tensor(zs[a][:, t, :], h[t][:].indirect(cen_sb[:, lst]), both[t][a][:], ADD)
+                if a == 0 and t < 2:
+                    last = PACK - 1
+                    nc.vector.tensor_tensor(both[last][t][:], first[:, last, halves[t]], second[:, last, halves[t]], ADD)
         banks = {}
         for a in range(2):
             z_bf = keep.tile([P, HALF, PACK], BF16, name="z_bf%d" % a, align_bytes=64)
@@ -147,7 +166,7 @@ def tile_picked_zgcnii_none_po_kernel(
             nc.vector.quantize_mx(out=z_words[:].bitcast(FP8X4), scales=z_scales[:], in_=z_bf[:].rearrange("p c t -> p (c t)"))
             for t in range(PACK):
                 rows = slice(P * t, P * (t + 1))
-                banks[a, t] = psum.tile([P, 512], F32, name="bank", tag="bank%d" % (PACK * a + t))
+                banks[a, t] = psum.tile([P, 512], F32, name="bank", tag="bank%d" % (PACK * (1 - a) + t))
                 nc.tensor.matmul_mx(
                     out=banks[a, t][:, :HALF], lhsT=w2w[:, rows].bitcast(FP8X4), lhsT_scale=w2s[:, rows],
                     rhs=z_words[:].bitcast(FP8X4), rhs_scale=z_scales[:], start=True, stop=True,

@@ -36,8 +36,8 @@ def tile_picked_zgcnii_none_po_kernel(
         pos2_sb = keep.tile([P, V // 16], U16, name="pos2_sb")
         xs_all = shared.tile([P, T], U8, name="xs_all", align_bytes=64, offset=0)
         xw_all = shared.tile([P, T], I32, name="xw_all", align_bytes=64, offset=2048)
-        w1_raw = [shared.tile([P, PACK, H // 2], F32, name="w1_raw%d" % c, align_bytes=64, offset=10240 + 4096 * c) for c in range(2)]
-        w2s_raw = keep.tile([P, H], U8, name="w2s_raw", align_bytes=64)
+        w1_raw = [shared.tile([P, PACK, H // 2], F32, name="w1_raw%d" % c, align_bytes=64, offset=14336 - 4096 * c) for c in range(2)]
+        w2s_raw = shared.tile([P, H], U8, name="w2s_raw", align_bytes=64, offset=18432)
         turn_raw = keep.tile([P, PACK], F32, name="turn_raw", align_bytes=64)
 
         nc.vector.memset(xs_all[:].bitcast(I32), 0)
@@ -48,21 +48,18 @@ def tile_picked_zgcnii_none_po_kernel(
         nc.sync.dma_start(pos2_sb[:], pos2)
         nc.sync.dma_start(w1_raw[0][:], w1_rows[:, :, : H // 2])
         nc.sync.dma_start(w1_raw[1][:], w1_rows[:, :, H // 2 :])
-        nc.sync.dma_start(cen_sb[:], cen)
         nc.sync.dma_start(xw_all[:], x_words[0].rearrange("p n t -> p (n t)").bitcast(I32))
+        nc.sync.dma_start(cen_sb[:], cen)
         for q in range(4):
             nc.scalar.dma_start(xs_all[32 * q : 32 * q + 4, :].bitcast(I32), x_scales[0, 4 * q : 4 * q + 4, :].bitcast(I32))
-        nc.gpsimd.dma_start(turn_raw[:], turn.rearrange("(p t) o -> p (t o)", t=PACK))
         for q in range(4):
             nc.gpsimd.dma_start(w2s_raw[32 * q : 32 * q + 4, :].bitcast(I32), w2_scales[0, 4 * q : 4 * q + 4, :].bitcast(I32))
         ident = keep.tile([P, P], F32, name="ident", align_bytes=64)
         make_identity(nc, ident[:])
+        nc.gpsimd.dma_start(turn_raw[:], turn.rearrange("(p t) o -> p (t o)", t=PACK))
 
         turn_sc = keep.tile([P, PACK], F32, name="turn_sc", align_bytes=64)
         nc.gpsimd.tensor_scalar(turn_sc[:], turn_raw[:], 0.4, 0.0, MULT, ADD)
-
-        xq_scales = keep.tile([P, S], U8, name="xq_scales", align_bytes=64)
-        nc.vector.tensor_copy(xq_scales[:], xs_all[:].indirect(offs_sb[:]))
 
         w1_words = keep.tile([P, H], U32, name="w1_words", align_bytes=64)
         w1_scales = keep.tile([P, H], U8, name="w1_scales", align_bytes=64)
@@ -78,13 +75,13 @@ def tile_picked_zgcnii_none_po_kernel(
                 nc.vector.quantize_mx(
                     out=w1_words[:, cols].bitcast(FP8X4), scales=w1_scales[:, cols], in_=w1_bf[:, t].rearrange("p m j -> p (m j)")
                 )
-        gate_raw = shared.tile([P, 2, V], F32, name="gate_raw", align_bytes=64, offset=10240)
-        nc.sync.dma_start(gate_raw[:], gate.rearrange("d p v -> p d v"))
-        w2w_raw = shared.tile([P, H], I32, name="w2w_raw", align_bytes=64, offset=12288)
-        nc.sync.dma_start(w2w_raw[:], w2_words[0].rearrange("p n t -> p (n t)").bitcast(I32))
+        xq_scales = keep.tile([P, S], U8, name="xq_scales", align_bytes=64)
+        nc.vector.tensor_copy(xq_scales[:], xs_all[:].indirect(offs_sb[:]))
 
-        gate_sc = shared.tile([P, 2, V], F32, name="gate_sc", align_bytes=64, offset=14336)
-        nc.scalar.activation(gate_sc[:], gate_raw[:], COPY, scale=9.0)
+        w2w_raw = shared.tile([P, H], I32, name="w2w_raw", align_bytes=64, offset=16384)
+        nc.sync.dma_start(w2w_raw[:], w2_words[0].rearrange("p n t -> p (n t)").bitcast(I32))
+        gate_sb = shared.tile([P, 2, V], F32, name="gate_sb", align_bytes=64, offset=14336)
+        nc.sync.dma_start(gate_sb[:], gate.rearrange("d p v -> p d v"))
 
         xq_words = shared.tile([P, S], U32, name="xq_words", align_bytes=64, offset=0)
         for c in range(2):
@@ -101,7 +98,6 @@ def tile_picked_zgcnii_none_po_kernel(
             )
             nc.scalar.activation(h[t][:, lo:hi], bank[:, : hi - lo], COPY, scale=0.06)
 
-
         w2w = shared.tile([P, H], U32, name="w2w", align_bytes=64, offset=4096)
         nc.vector.tensor_copy(
             w2w[:].rearrange("p (t a b) -> p a t b", t=PACK, b=4),
@@ -113,45 +109,55 @@ def tile_picked_zgcnii_none_po_kernel(
             w2s_raw[:].rearrange("p (a b t) -> p a t b", t=PACK, b=16),
         )
 
-        first = keep.tile([P, PACK, V], F32, name="first", align_bytes=64)
+        gate9 = shared.tile([P, 2, V], F32, name="gate9", align_bytes=64, offset=0)
+        nc.scalar.activation(gate9[:], gate_sb[:], COPY, scale=9.0)
+
+        first = shared.tile([P, PACK, V], F32, name="first", align_bytes=64, offset=16384)
         second = keep.tile([P, PACK, V], F32, name="second", align_bytes=64)
-        both = [
-            [
-                shared.tile([P, HALF], F32, name="both%d_0" % t, align_bytes=64, offset=8192 + 512 * t),
-                keep.tile([P, HALF], F32, name="both%d_1" % t, align_bytes=64),
-            ]
-            for t in range(PACK)
-        ]
         halves = [slice(HALF * a, HALF * (a + 1)) for a in range(2)]
+        lists = [slice(HALF // 16 * a, HALF // 16 * (a + 1)) for a in range(2)]
+        last = PACK - 1
+        both0 = keep.tile([P, V], F32, name="both0", align_bytes=64)
+        both1 = shared.tile([P, V], F32, name="both1", align_bytes=64, offset=2048)
+        both2 = [
+            shared.tile([P, HALF], F32, name="both2_0", align_bytes=64, offset=8192),
+            keep.tile([P, HALF], F32, name="both2_1", align_bytes=64),
+        ]
+        both3 = keep.tile([P, V], F32, name="both3", align_bytes=64)
+        both = [[both0[:, c] for c in halves], [both1[:, c] for c in halves], [b[:] for b in both2], [both3[:, c] for c in halves]]
         for t in range(PACK):
-            nc.vector.tensor_tensor(first[:, t, :], h[t][:].indirect(pos1_sb[:]), gate_sc[:, 0, :], MULT)
-            nc.vector.tensor_tensor(second[:, t, :], h[t][:].indirect(pos2_sb[:]), gate_sc[:, 1, :], MULT)
-            if t < PACK - 1:
-                turn_banks = [psum.tile([P, 512], F32, name="bank", tag="bank%d" % ((2 * t + a + 6) % 8)) for a in range(2)]
-                turned = [keep.tile([P, P], F32, name="turned%d_%d" % (t, a), align_bytes=64) for a in range(2)]
+            gates = gate9 if t == last else gate_sb
+            nc.vector.tensor_tensor(first[:, t, :], h[t][:].indirect(pos1_sb[:]), gates[:, 0, :], MULT)
+            nc.vector.tensor_tensor(second[:, t, :], h[t][:].indirect(pos2_sb[:]), gates[:, 1, :], MULT)
+            if t < last:
+                there = psum.tile([P, 512], F32, name="bank", tag="bank6")
                 for a in range(2):
-                    nc.tensor.matmul(turn_banks[a][:, :P], first[:, t, halves[a]], ident[:], start=True, stop=False, is_transpose=True)
-                    nc.tensor.matmul(turn_banks[a][:, :P], second[:, t, halves[a]], ident[:], start=False, stop=True, is_transpose=True)
-                    nc.scalar.copy(turned[a][:], turn_banks[a][:, :P])
+                    nc.tensor.matmul(there[:, halves[a]], first[:, t, halves[a]], ident[:], start=True, stop=False, is_transpose=True)
+                    nc.tensor.matmul(there[:, halves[a]], second[:, t, halves[a]], ident[:], start=False, stop=True, is_transpose=True)
+                turned = keep.tile([P, V], F32, name="turned%d" % t, align_bytes=64)
+                nc.scalar.copy(turned[:], there[:, :V])
+                back = psum.tile([P, 512], F32, name="bank", tag="bank7")
                 for a in range(2):
-                    nc.tensor.transpose(turn_banks[a][:, P : 2 * P], turned[a][:], ident[:])
-                    nc.scalar.copy(both[t][a][:], turn_banks[a][:, P : 2 * P])
+                    nc.tensor.transpose(back[:, halves[a]], turned[:, halves[a]], ident[:])
+                if t < 2:
+                    nc.scalar.activation((both0, both1)[t][:], back[:, :V], COPY, scale=9.0)
+                else:
+                    for a in range(2):
+                        nc.scalar.activation(both[t][a], back[:, halves[a]], COPY, scale=9.0)
 
         o_words = keep.tile([P, V], I32, name="o_words", align_bytes=64)
         o_scales = keep.tile([P, V], U8, name="o_scales", align_bytes=64)
         out_rows = out_0.rearrange("(p t) v -> p t v", t=PACK)
         out_words = out_1[0].rearrange("p n t -> p (n t)").bitcast(I32)
         zs = [
-            shared.tile([P, PACK, HALF], F32, name="zs0", align_bytes=64, offset=14336),
+            keep.tile([P, PACK, HALF], F32, name="zs0", align_bytes=64),
             shared.tile([P, PACK, HALF], F32, name="zs1", align_bytes=64, offset=8192),
         ]
         for a in range(2):
-            lst = slice(HALF // 16 * a, HALF // 16 * (a + 1))
-            for t in range(PACK):
-                nc.vector.tensor_tensor(zs[a][:, t, :], h[t][:].indirect(cen_sb[:, lst]), both[t][a][:], ADD)
-                if a == 0 and t < 2:
-                    last = PACK - 1
-                    nc.vector.tensor_tensor(both[last][t][:], first[:, last, halves[t]], second[:, last, halves[t]], ADD)
+            for t in ((0, 1, 3, 2), (0, 1, 2, 3))[a]:
+                nc.vector.tensor_tensor(zs[a][:, t, :], h[t][:].indirect(cen_sb[:, lists[a]]), both[t][a], ADD)
+                if (a, t) == (0, 0):
+                    nc.vector.tensor_tensor(both3[:], first[:, last, :], second[:, last, :], ADD)
         banks = {}
         for a in range(2):
             z_bf = keep.tile([P, HALF, PACK], BF16, name="z_bf%d" % a, align_bytes=64)
@@ -161,7 +167,7 @@ def tile_picked_zgcnii_none_po_kernel(
                 nc.scalar.activation(woven, planes, COPY, scale=1.0 / 0.6)
             else:
                 nc.vector.tensor_scalar_mul(woven, planes, 1.0 / 0.6)
-            z_words = keep.tile([P, HALF], U32, name="z_words%d" % a, align_bytes=64)
+            z_words = shared.tile([P, HALF], U32, name="z_words%d" % a, align_bytes=64, offset=2048 + 1024 * a)
             z_scales = keep.tile([P, HALF], U8, name="z_scales%d" % a, align_bytes=64)
             nc.vector.quantize_mx(out=z_words[:].bitcast(FP8X4), scales=z_scales[:], in_=z_bf[:].rearrange("p c t -> p (c t)"))
             for t in range(PACK):

@@ -48,18 +48,21 @@ def tile_picked_zgcnii_none_po_kernel(
         nc.sync.dma_start(pos2_sb[:], pos2)
         nc.sync.dma_start(w1_raw[0][:], w1_rows[:, :, : H // 2])
         nc.sync.dma_start(w1_raw[1][:], w1_rows[:, :, H // 2 :])
-        nc.sync.dma_start(xw_all[:], x_words[0].rearrange("p n t -> p (n t)").bitcast(I32))
         nc.sync.dma_start(cen_sb[:], cen)
+        nc.sync.dma_start(xw_all[:], x_words[0].rearrange("p n t -> p (n t)").bitcast(I32))
         for q in range(4):
             nc.scalar.dma_start(xs_all[32 * q : 32 * q + 4, :].bitcast(I32), x_scales[0, 4 * q : 4 * q + 4, :].bitcast(I32))
+        nc.gpsimd.dma_start(turn_raw[:], turn.rearrange("(p t) o -> p (t o)", t=PACK))
         for q in range(4):
             nc.gpsimd.dma_start(w2s_raw[32 * q : 32 * q + 4, :].bitcast(I32), w2_scales[0, 4 * q : 4 * q + 4, :].bitcast(I32))
         ident = keep.tile([P, P], F32, name="ident", align_bytes=64)
         make_identity(nc, ident[:])
-        nc.gpsimd.dma_start(turn_raw[:], turn.rearrange("(p t) o -> p (t o)", t=PACK))
 
         turn_sc = keep.tile([P, PACK], F32, name="turn_sc", align_bytes=64)
         nc.gpsimd.tensor_scalar(turn_sc[:], turn_raw[:], 0.4, 0.0, MULT, ADD)
+
+        xq_scales = keep.tile([P, S], U8, name="xq_scales", align_bytes=64)
+        nc.vector.tensor_copy(xq_scales[:], xs_all[:].indirect(offs_sb[:]))
 
         w1_words = keep.tile([P, H], U32, name="w1_words", align_bytes=64)
         w1_scales = keep.tile([P, H], U8, name="w1_scales", align_bytes=64)
@@ -75,13 +78,11 @@ def tile_picked_zgcnii_none_po_kernel(
                 nc.vector.quantize_mx(
                     out=w1_words[:, cols].bitcast(FP8X4), scales=w1_scales[:, cols], in_=w1_bf[:, t].rearrange("p m j -> p (m j)")
                 )
-        xq_scales = keep.tile([P, S], U8, name="xq_scales", align_bytes=64)
-        nc.vector.tensor_copy(xq_scales[:], xs_all[:].indirect(offs_sb[:]))
 
-        w2w_raw = shared.tile([P, H], I32, name="w2w_raw", align_bytes=64, offset=16384)
-        nc.sync.dma_start(w2w_raw[:], w2_words[0].rearrange("p n t -> p (n t)").bitcast(I32))
         gate_sb = shared.tile([P, 2, V], F32, name="gate_sb", align_bytes=64, offset=14336)
         nc.sync.dma_start(gate_sb[:], gate.rearrange("d p v -> p d v"))
+        w2w_raw = shared.tile([P, H], I32, name="w2w_raw", align_bytes=64, offset=16384)
+        nc.sync.dma_start(w2w_raw[:], w2_words[0].rearrange("p n t -> p (n t)").bitcast(I32))
 
         xq_words = shared.tile([P, S], U32, name="xq_words", align_bytes=64, offset=0)
         for c in range(2):
@@ -112,7 +113,7 @@ def tile_picked_zgcnii_none_po_kernel(
         gate9 = shared.tile([P, 2, V], F32, name="gate9", align_bytes=64, offset=0)
         nc.scalar.activation(gate9[:], gate_sb[:], COPY, scale=9.0)
 
-        first = shared.tile([P, PACK, V], F32, name="first", align_bytes=64, offset=16384)
+        first = keep.tile([P, PACK, V], F32, name="first", align_bytes=64)
         second = keep.tile([P, PACK, V], F32, name="second", align_bytes=64)
         halves = [slice(HALF * a, HALF * (a + 1)) for a in range(2)]
         lists = [slice(HALF // 16 * a, HALF // 16 * (a + 1)) for a in range(2)]

@@ -37,11 +37,8 @@ def tile_picked_zgcnii_none_po_kernel(
         xs_all = shared.tile([P, T], U8, name="xs_all", align_bytes=64, offset=0)
         xw_all = shared.tile([P, T], I32, name="xw_all", align_bytes=64, offset=2048)
         w1_raw = [shared.tile([P, PACK, H // 2], F32, name="w1_raw%d" % c, align_bytes=64, offset=14336 - 4096 * c) for c in range(2)]
-        w2s_raw = shared.tile([P, H], U8, name="w2s_raw", align_bytes=64, offset=18432)
-        turn_raw = keep.tile([P, PACK], F32, name="turn_raw", align_bytes=64)
 
         nc.vector.memset(xs_all[:].bitcast(I32), 0)
-        nc.gpsimd.memset(w2s_raw[:].bitcast(I32), 0)
         w1_rows = w1.rearrange("(p j) c -> p j c", j=PACK)
         nc.sync.dma_start(offs_sb[:], offs)
         nc.sync.dma_start(pos1_sb[:], pos1)
@@ -52,14 +49,8 @@ def tile_picked_zgcnii_none_po_kernel(
         nc.sync.dma_start(xw_all[:], x_words[0].rearrange("p n t -> p (n t)").bitcast(I32))
         for q in range(4):
             nc.scalar.dma_start(xs_all[32 * q : 32 * q + 4, :].bitcast(I32), x_scales[0, 4 * q : 4 * q + 4, :].bitcast(I32))
-        nc.gpsimd.dma_start(turn_raw[:], turn.rearrange("(p t) o -> p (t o)", t=PACK))
-        for q in range(4):
-            nc.gpsimd.dma_start(w2s_raw[32 * q : 32 * q + 4, :].bitcast(I32), w2_scales[0, 4 * q : 4 * q + 4, :].bitcast(I32))
         ident = keep.tile([P, P], F32, name="ident", align_bytes=64)
         make_identity(nc, ident[:])
-
-        turn_sc = keep.tile([P, PACK], F32, name="turn_sc", align_bytes=64)
-        nc.gpsimd.tensor_scalar(turn_sc[:], turn_raw[:], 0.4, 0.0, MULT, ADD)
 
         xq_scales = keep.tile([P, S], U8, name="xq_scales", align_bytes=64)
         nc.vector.tensor_copy(xq_scales[:], xs_all[:].indirect(offs_sb[:]))
@@ -88,6 +79,13 @@ def tile_picked_zgcnii_none_po_kernel(
         for c in range(2):
             nc.vector.tensor_copy(xq_words[:, 256 * c : 256 * (c + 1)], xw_all[:].bitcast(U32).indirect(offs_sb[:, 16 * c : 16 * (c + 1)]))
 
+        w2s_raw = shared.tile([P, H], U8, name="w2s_raw", align_bytes=64, offset=6656)
+        nc.vector.memset(w2s_raw[:].bitcast(I32), 0)
+        for q in range(4):
+            nc.sync.dma_start(w2s_raw[32 * q : 32 * q + 4, :].bitcast(I32), w2_scales[0, 4 * q : 4 * q + 4, :].bitcast(I32))
+        turn_raw = shared.tile([P, PACK], F32, name="turn_raw", align_bytes=64, offset=7168)
+        nc.sync.dma_start(turn_raw[:], turn.rearrange("(p t) o -> p (t o)", t=PACK))
+
         h = [keep.tile([P, S], F32, name="h%d" % t, align_bytes=64) for t in range(PACK)]
         pieces = [(0, 0, 256), (0, 256, 384), (0, 384, 512)] + [(t, 0, S) for t in range(1, PACK)]
         for n, (t, lo, hi) in enumerate(pieces):
@@ -110,7 +108,7 @@ def tile_picked_zgcnii_none_po_kernel(
             w2s_raw[:].rearrange("p (a b t) -> p a t b", t=PACK, b=16),
         )
 
-        gate9 = shared.tile([P, 2, V], F32, name="gate9", align_bytes=64, offset=0)
+        gate9 = keep.tile([P, 2, V], F32, name="gate9", align_bytes=64)
         nc.scalar.activation(gate9[:], gate_sb[:], COPY, scale=9.0)
 
         first = keep.tile([P, PACK, V], F32, name="first", align_bytes=64)
@@ -118,33 +116,31 @@ def tile_picked_zgcnii_none_po_kernel(
         halves = [slice(HALF * a, HALF * (a + 1)) for a in range(2)]
         lists = [slice(HALF // 16 * a, HALF // 16 * (a + 1)) for a in range(2)]
         last = PACK - 1
-        both0 = keep.tile([P, V], F32, name="both0", align_bytes=64)
-        both1 = shared.tile([P, V], F32, name="both1", align_bytes=64, offset=2048)
-        both2 = [
-            shared.tile([P, HALF], F32, name="both2_0", align_bytes=64, offset=8192),
-            keep.tile([P, HALF], F32, name="both2_1", align_bytes=64),
+        both = [
+            [
+                shared.tile([P, HALF], F32, name="both%d_0" % t, align_bytes=64, offset=8192 + 512 * t)[:],
+                shared.tile([P, HALF], F32, name="both%d_1" % t, align_bytes=64, offset=10240 + 512 * t)[:],
+            ]
+            for t in range(last)
         ]
         both3 = keep.tile([P, V], F32, name="both3", align_bytes=64)
-        both = [[both0[:, c] for c in halves], [both1[:, c] for c in halves], [b[:] for b in both2], [both3[:, c] for c in halves]]
+        both.append([both3[:, c] for c in halves])
         for t in range(PACK):
             gates = gate9 if t == last else gate_sb
             nc.vector.tensor_tensor(first[:, t, :], h[t][:].indirect(pos1_sb[:]), gates[:, 0, :], MULT)
             nc.vector.tensor_tensor(second[:, t, :], h[t][:].indirect(pos2_sb[:]), gates[:, 1, :], MULT)
             if t < last:
-                there = psum.tile([P, 512], F32, name="bank", tag="bank6")
+                turn_banks = [psum.tile([P, 512], F32, name="bank", tag="bank%d" % ((2 * t + a + 6) % 8)) for a in range(2)]
+                turned = [shared.tile([P, P], F32, name="turned%d_%d" % (t, a), align_bytes=64, offset=20480 + 512 * (2 * t + a)) for a in range(2)]
                 for a in range(2):
-                    nc.tensor.matmul(there[:, halves[a]], first[:, t, halves[a]], ident[:], start=True, stop=False, is_transpose=True)
-                    nc.tensor.matmul(there[:, halves[a]], second[:, t, halves[a]], ident[:], start=False, stop=True, is_transpose=True)
-                turned = keep.tile([P, V], F32, name="turned%d" % t, align_bytes=64)
-                nc.scalar.copy(turned[:], there[:, :V])
-                back = psum.tile([P, 512], F32, name="bank", tag="bank7")
+                    nc.tensor.matmul(turn_banks[a][:, :P], first[:, t, halves[a]], ident[:], start=True, stop=False, is_transpose=True)
+                    nc.tensor.matmul(turn_banks[a][:, :P], second[:, t, halves[a]], ident[:], start=False, stop=True, is_transpose=True)
+                    nc.scalar.copy(turned[a][:], turn_banks[a][:, :P])
                 for a in range(2):
-                    nc.tensor.transpose(back[:, halves[a]], turned[:, halves[a]], ident[:])
-                if t < 2:
-                    nc.scalar.activation((both0, both1)[t][:], back[:, :V], COPY, scale=9.0)
-                else:
-                    for a in range(2):
-                        nc.scalar.activation(both[t][a], back[:, halves[a]], COPY, scale=9.0)
+                    nc.tensor.transpose(turn_banks[a][:, P : 2 * P], turned[a][:], ident[:])
+                    nc.scalar.activation(both[t][a], turn_banks[a][:, P : 2 * P], COPY, scale=9.0)
+        turn_sc = shared.tile([P, PACK], F32, name="turn_sc", align_bytes=64, offset=20480 + 512 * 5)
+        nc.scalar.activation(turn_sc[:], turn_raw[:], COPY, scale=0.4)
 
         o_words = keep.tile([P, V], I32, name="o_words", align_bytes=64)
         o_scales = keep.tile([P, V], U8, name="o_scales", align_bytes=64)
@@ -168,7 +164,7 @@ def tile_picked_zgcnii_none_po_kernel(
                 nc.scalar.activation(woven, planes, COPY, scale=1.0 / 0.6)
             else:
                 nc.vector.tensor_scalar_mul(woven, planes, 1.0 / 0.6)
-            z_words = shared.tile([P, HALF], U32, name="z_words%d" % a, align_bytes=64, offset=2048 + 1024 * a)
+            z_words = shared.tile([P, HALF], U32, name="z_words%d" % a, align_bytes=64, offset=10752 + 1024 * a)
             z_scales = keep.tile([P, HALF], U8, name="z_scales%d" % a, align_bytes=64)
             nc.vector.quantize_mx(out=z_words[:].bitcast(FP8X4), scales=z_scales[:], in_=z_bf[:].rearrange("p c t -> p (c t)"))
             for t in range(PACK):

@@ -36,7 +36,7 @@ def tile_picked_zgcnii_none_po_kernel(
         pos2_sb = keep.tile([P, V // 16], U16, name="pos2_sb")
         xs_all = shared.tile([P, T], U8, name="xs_all", align_bytes=64, offset=0)
         xw_all = shared.tile([P, T], I32, name="xw_all", align_bytes=64, offset=2048)
-        w1_raw = [shared.tile([P, PACK, H // 2], F32, name="w1_raw%d" % c, align_bytes=64, offset=14336 - 4096 * c) for c in range(2)]
+        w1_raw = [shared.tile([P, PACK, H // 2], F32, name="w1_raw%d" % c, align_bytes=64, offset=14336 + 12288 * c) for c in range(2)]
 
         nc.vector.memset(xs_all[:].bitcast(I32), 0)
         w1_rows = w1.rearrange("(p j) c -> p j c", j=PACK)
@@ -70,19 +70,19 @@ def tile_picked_zgcnii_none_po_kernel(
                     out=w1_words[:, cols].bitcast(FP8X4), scales=w1_scales[:, cols], in_=w1_bf[:, t].rearrange("p m j -> p (m j)")
                 )
 
-        gate_sb = shared.tile([P, 2, V], F32, name="gate_sb", align_bytes=64, offset=14336)
-        nc.sync.dma_start(gate_sb[:], gate.rearrange("d p v -> p d v"))
-        w2w_raw = shared.tile([P, H], I32, name="w2w_raw", align_bytes=64, offset=16384)
+        w2s_raw = shared.tile([P, H], U8, name="w2s_raw", align_bytes=64, offset=18304)
+        nc.gpsimd.memset(w2s_raw[:].bitcast(I32), 0)
+        for q in range(4):
+            nc.sync.dma_start(w2s_raw[32 * q : 32 * q + 4, :].bitcast(I32), w2_scales[0, 4 * q : 4 * q + 4, :].bitcast(I32))
+        w2w_raw = shared.tile([P, H], I32, name="w2w_raw", align_bytes=64, offset=14592)
         nc.sync.dma_start(w2w_raw[:], w2_words[0].rearrange("p n t -> p (n t)").bitcast(I32))
+        gate_sb = shared.tile([P, 2, V], F32, name="gate_sb", align_bytes=64, offset=12544)
+        nc.sync.dma_start(gate_sb[:], gate.rearrange("d p v -> p d v"))
 
         xq_words = shared.tile([P, S], U32, name="xq_words", align_bytes=64, offset=0)
         for c in range(2):
             nc.vector.tensor_copy(xq_words[:, 256 * c : 256 * (c + 1)], xw_all[:].bitcast(U32).indirect(offs_sb[:, 16 * c : 16 * (c + 1)]))
 
-        w2s_raw = shared.tile([P, H], U8, name="w2s_raw", align_bytes=64, offset=6656)
-        nc.vector.memset(w2s_raw[:].bitcast(I32), 0)
-        for q in range(4):
-            nc.sync.dma_start(w2s_raw[32 * q : 32 * q + 4, :].bitcast(I32), w2_scales[0, 4 * q : 4 * q + 4, :].bitcast(I32))
         turn_raw = shared.tile([P, PACK], F32, name="turn_raw", align_bytes=64, offset=7168)
         nc.sync.dma_start(turn_raw[:], turn.rearrange("(p t) o -> p (t o)", t=PACK))
 
@@ -108,11 +108,11 @@ def tile_picked_zgcnii_none_po_kernel(
             w2s_raw[:].rearrange("p (a b t) -> p a t b", t=PACK, b=16),
         )
 
-        gate9 = keep.tile([P, 2, V], F32, name="gate9", align_bytes=64)
+        gate9 = shared.tile([P, 2, V], F32, name="gate9", align_bytes=64, offset=0)
         nc.scalar.activation(gate9[:], gate_sb[:], COPY, scale=9.0)
 
-        first = keep.tile([P, PACK, V], F32, name="first", align_bytes=64)
-        second = keep.tile([P, PACK, V], F32, name="second", align_bytes=64)
+        first = shared.tile([P, PACK, V], F32, name="first", align_bytes=64, offset=14592)
+        second = shared.tile([P, PACK, V], F32, name="second", align_bytes=64, offset=18688)
         halves = [slice(HALF * a, HALF * (a + 1)) for a in range(2)]
         lists = [slice(HALF // 16 * a, HALF // 16 * (a + 1)) for a in range(2)]
         last = PACK - 1
@@ -131,7 +131,7 @@ def tile_picked_zgcnii_none_po_kernel(
             nc.vector.tensor_tensor(second[:, t, :], h[t][:].indirect(pos2_sb[:]), gates[:, 1, :], MULT)
             if t < last:
                 turn_banks = [psum.tile([P, 512], F32, name="bank", tag="bank%d" % ((2 * t + a + 6) % 8)) for a in range(2)]
-                turned = [shared.tile([P, P], F32, name="turned%d_%d" % (t, a), align_bytes=64, offset=20480 + 512 * (2 * t + a)) for a in range(2)]
+                turned = [shared.tile([P, P], F32, name="turned%d_%d" % (t, a), align_bytes=64, offset=23040 + 512 * (2 * t + a)) for a in range(2)]
                 for a in range(2):
                     nc.tensor.matmul(turn_banks[a][:, :P], first[:, t, halves[a]], ident[:], start=True, stop=False, is_transpose=True)
                     nc.tensor.matmul(turn_banks[a][:, :P], second[:, t, halves[a]], ident[:], start=False, stop=True, is_transpose=True)
@@ -139,7 +139,7 @@ def tile_picked_zgcnii_none_po_kernel(
                 for a in range(2):
                     nc.tensor.transpose(turn_banks[a][:, P : 2 * P], turned[a][:], ident[:])
                     nc.scalar.activation(both[t][a], turn_banks[a][:, P : 2 * P], COPY, scale=9.0)
-        turn_sc = shared.tile([P, PACK], F32, name="turn_sc", align_bytes=64, offset=20480 + 512 * 5)
+        turn_sc = shared.tile([P, PACK], F32, name="turn_sc", align_bytes=64, offset=23040 + 512 * 5)
         nc.scalar.activation(turn_sc[:], turn_raw[:], COPY, scale=0.4)
 
         o_words = keep.tile([P, V], I32, name="o_words", align_bytes=64)

@@ -42,13 +42,14 @@ def tile_picked_zgcnii_none_po_kernel(
         w1_rows = w1.rearrange("(p j) c -> p j c", j=PACK)
         nc.sync.dma_start(offs_sb[:], offs)
         nc.sync.dma_start(pos1_sb[:], pos1)
-        nc.sync.dma_start(pos2_sb[:], pos2)
         nc.sync.dma_start(w1_raw[0][:], w1_rows[:, :, : H // 2])
-        nc.sync.dma_start(w1_raw[1][:], w1_rows[:, :, H // 2 :])
-        nc.sync.dma_start(cen_sb[:], cen)
-        nc.sync.dma_start(xw_all[:], x_words[0].rearrange("p n t -> p (n t)").bitcast(I32))
         for q in range(4):
-            nc.scalar.dma_start(xs_all[32 * q : 32 * q + 4, :].bitcast(I32), x_scales[0, 4 * q : 4 * q + 4, :].bitcast(I32))
+            eng = nc.scalar if q < 2 else nc.sync
+            eng.dma_start(xs_all[32 * q : 32 * q + 4, :].bitcast(I32), x_scales[0, 4 * q : 4 * q + 4, :].bitcast(I32))
+        nc.sync.dma_start(w1_raw[1][:], w1_rows[:, :, H // 2 :])
+        nc.sync.dma_start(pos2_sb[:], pos2)
+        nc.sync.dma_start(xw_all[:], x_words[0].rearrange("p n t -> p (n t)").bitcast(I32))
+        nc.sync.dma_start(cen_sb[:], cen)
         ident = keep.tile([P, P], F32, name="ident", align_bytes=64)
         make_identity(nc, ident[:])
 
@@ -163,7 +164,8 @@ def tile_picked_zgcnii_none_po_kernel(
             if a == 0:
                 nc.scalar.activation(woven, planes, COPY, scale=1.0 / 0.6)
             else:
-                nc.vector.tensor_scalar_mul(woven, planes, 1.0 / 0.6)
+                nc.vector.tensor_scalar_mul(woven[:, :20], planes[:, :20], 1.0 / 0.6)
+                nc.scalar.activation(woven[:, 20:], planes[:, 20:], COPY, scale=1.0 / 0.6)
             z_words = shared.tile([P, HALF], U32, name="z_words%d" % a, align_bytes=64, offset=10752 + 1024 * a)
             z_scales = keep.tile([P, HALF], U8, name="z_scales%d" % a, align_bytes=64)
             nc.vector.quantize_mx(out=z_words[:].bitcast(FP8X4), scales=z_scales[:], in_=z_bf[:].rearrange("p c t -> p (c t)"))

@@ -36,19 +36,27 @@ def tile_picked_zgcnii_none_po_kernel(
         pos2_sb = keep.tile([P, V // 16], U16, name="pos2_sb")
         xs_all = shared.tile([P, T], U8, name="xs_all", align_bytes=64, offset=0)
         xw_all = shared.tile([P, T], I32, name="xw_all", align_bytes=64, offset=2048)
-        w1_raw = [shared.tile([P, PACK, H // 2], F32, name="w1_raw%d" % c, align_bytes=64, offset=14336 + 12288 * c) for c in range(2)]
+        w1_raw = [shared.tile([P, PACK, H // 2], F32, name="w1_raw%d" % c, align_bytes=64, offset=32768 + 4096 * c) for c in range(2)]
 
         nc.vector.memset(xs_all[:].bitcast(I32), 0)
         w1_rows = w1.rearrange("(p j) c -> p j c", j=PACK)
+        w2s_raw = shared.tile([P, H], U8, name="w2s_raw", align_bytes=64, offset=18304)
+        nc.vector.memset(w2s_raw[:].bitcast(I32), 0)
         nc.sync.dma_start(offs_sb[:], offs)
-        nc.sync.dma_start(pos1_sb[:], pos1)
         nc.sync.dma_start(w1_raw[0][:], w1_rows[:, :, : H // 2])
         for q in range(4):
             eng = nc.scalar if q < 2 else nc.sync
             eng.dma_start(xs_all[32 * q : 32 * q + 4, :].bitcast(I32), x_scales[0, 4 * q : 4 * q + 4, :].bitcast(I32))
+        nc.sync.dma_start(pos1_sb[:], pos1)
+        nc.sync.dma_start(xw_all[:], x_words[0].rearrange("p n t -> p (n t)").bitcast(I32))
         nc.sync.dma_start(w1_raw[1][:], w1_rows[:, :, H // 2 :])
         nc.sync.dma_start(pos2_sb[:], pos2)
-        nc.sync.dma_start(xw_all[:], x_words[0].rearrange("p n t -> p (n t)").bitcast(I32))
+        for q in range(4):
+            nc.sync.dma_start(w2s_raw[32 * q : 32 * q + 4, :].bitcast(I32), w2_scales[0, 4 * q : 4 * q + 4, :].bitcast(I32))
+        w2w_raw = shared.tile([P, H], I32, name="w2w_raw", align_bytes=64, offset=14592)
+        nc.sync.dma_start(w2w_raw[:], w2_words[0].rearrange("p n t -> p (n t)").bitcast(I32))
+        gate_sb = shared.tile([P, 2, V], F32, name="gate_sb", align_bytes=64, offset=12544)
+        nc.sync.dma_start(gate_sb[:], gate.rearrange("d p v -> p d v"))
         nc.sync.dma_start(cen_sb[:], cen)
         ident = keep.tile([P, P], F32, name="ident", align_bytes=64)
         make_identity(nc, ident[:])
@@ -58,8 +66,12 @@ def tile_picked_zgcnii_none_po_kernel(
 
         w1_words = keep.tile([P, H], U32, name="w1_words", align_bytes=64)
         w1_scales = keep.tile([P, H], U8, name="w1_scales", align_bytes=64)
-        split = 40
+        xq_words = shared.tile([P, S], U32, name="xq_words", align_bytes=64, offset=0)
         for c in range(2):
+            if c == 1:
+                for g in range(2):
+                    nc.vector.tensor_copy(xq_words[:, 256 * g : 256 * (g + 1)], xw_all[:].bitcast(U32).indirect(offs_sb[:, 16 * g : 16 * (g + 1)]))
+            split = (40, 34)[c]
             w1_bf = keep.tile([P, PACK, P // 2, PACK], BF16, name="w1_bf%d" % c, align_bytes=64)
             src = w1_raw[c][:].rearrange("p j (m t) -> p m t j", t=PACK)
             dst = w1_bf[:].rearrange("p t m j -> p m t j")
@@ -71,24 +83,11 @@ def tile_picked_zgcnii_none_po_kernel(
                     out=w1_words[:, cols].bitcast(FP8X4), scales=w1_scales[:, cols], in_=w1_bf[:, t].rearrange("p m j -> p (m j)")
                 )
 
-        w2s_raw = shared.tile([P, H], U8, name="w2s_raw", align_bytes=64, offset=18304)
-        nc.gpsimd.memset(w2s_raw[:].bitcast(I32), 0)
-        for q in range(4):
-            nc.sync.dma_start(w2s_raw[32 * q : 32 * q + 4, :].bitcast(I32), w2_scales[0, 4 * q : 4 * q + 4, :].bitcast(I32))
-        w2w_raw = shared.tile([P, H], I32, name="w2w_raw", align_bytes=64, offset=14592)
-        nc.sync.dma_start(w2w_raw[:], w2_words[0].rearrange("p n t -> p (n t)").bitcast(I32))
-        gate_sb = shared.tile([P, 2, V], F32, name="gate_sb", align_bytes=64, offset=12544)
-        nc.sync.dma_start(gate_sb[:], gate.rearrange("d p v -> p d v"))
-
-        xq_words = shared.tile([P, S], U32, name="xq_words", align_bytes=64, offset=0)
-        for c in range(2):
-            nc.vector.tensor_copy(xq_words[:, 256 * c : 256 * (c + 1)], xw_all[:].bitcast(U32).indirect(offs_sb[:, 16 * c : 16 * (c + 1)]))
-
         turn_raw = shared.tile([P, PACK], F32, name="turn_raw", align_bytes=64, offset=7168)
         nc.sync.dma_start(turn_raw[:], turn.rearrange("(p t) o -> p (t o)", t=PACK))
 
         h = [keep.tile([P, S], F32, name="h%d" % t, align_bytes=64) for t in range(PACK)]
-        pieces = [(0, 0, 256), (0, 256, 384), (0, 384, 512)] + [(t, 0, S) for t in range(1, PACK)]
+        pieces = [(0, 0, 256), (0, 256, 512)] + [(t, 0, S) for t in range(1, PACK)]
         for n, (t, lo, hi) in enumerate(pieces):
             rows = slice(P * t, P * (t + 1))
             bank = psum.tile([P, 512], F32, name="bank", tag="bank%d" % n)

@@ -6,8 +6,30 @@ from concourse.masks import make_identity
 K, T, S, V, H = 512, 2048, 512, 256, 512
 P = 128
 PACK = 4
+QUADRANTS = 4
 HALF = V // 2
+PER_COLUMN = 16
+BANK = 512
+BANKS = 8
 FLOPS = 2 * K * H * S + 2 * H * H * V
+
+KEEP_Z, MIX_Y = 0.6, 0.4
+NEIGHBOURS, CENTRE = 0.9, 0.1
+
+CAST_STEPS = (((0, 4, 40),), ((0, 2, 32), (2, 4, 40)))
+WEAVE_ON_VECTOR = 20
+
+AT_X_SCALES = 0
+AT_X_WORDS = 2048
+AT_W2_WORDS = 4096
+AT_W2_SCALES = 6144
+AT_TURN = 7168
+AT_SUMS = (8192, 10240)
+AT_FIRST = 14592
+AT_SECOND = AT_FIRST + 4 * PACK * V
+AT_W2_SCALES_RAW = AT_SECOND - 384
+AT_TURNED = 23040
+HALF_PLANE = 4 * HALF
 
 F32 = mybir.dt.float32
 BF16 = mybir.dt.bfloat16
@@ -21,6 +43,22 @@ ADD = mybir.AluOpType.add
 COPY = mybir.ActivationFunctionType.Copy
 
 
+def scale_rows(tile, q):
+    return tile[32 * q : 32 * q + 4, :].bitcast(I32)
+
+
+def hbm_scale_rows(scales, q):
+    return scales[0, 4 * q : 4 * q + 4, :].bitcast(I32)
+
+
+def hbm_words(words):
+    return words[0].rearrange("p n r -> p (n r)").bitcast(I32)
+
+
+def weave_views(woven, planes):
+    return woven[:].rearrange("p (c i) t -> p c t i", i=4), planes[:].rearrange("p t (c i) -> p c t i", i=4)
+
+
 def tile_picked_zgcnii_none_po_kernel(
     tc, x_words, x_scales, w1, w2_words, w2_scales, gate, turn, offs, cen, pos1, pos2, out_0, out_1, out_2
 ):
@@ -30,168 +68,178 @@ def tile_picked_zgcnii_none_po_kernel(
         shared = ctx.enter_context(tc.tile_pool(name="shared", bufs=1))
         psum = ctx.enter_context(tc.psum_pool(name="psum", bufs=1))
 
-        offs_sb = keep.tile([P, S // 16], U16, name="offs_sb")
-        cen_sb = keep.tile([P, V // 16], U16, name="cen_sb")
-        pos1_sb = keep.tile([P, V // 16], U16, name="pos1_sb")
-        pos2_sb = keep.tile([P, V // 16], U16, name="pos2_sb")
-        xs_all = shared.tile([P, T], U8, name="xs_all", align_bytes=64, offset=0)
-        xw_all = shared.tile([P, T], I32, name="xw_all", align_bytes=64, offset=2048)
-        w1_raw = [shared.tile([P, PACK, H // 2], F32, name="w1_raw%d" % c, align_bytes=64, offset=32768 + 4096 * c) for c in range(2)]
+        def placed(shape, dtype, name, offset):
+            return shared.tile(shape, dtype, name=name, align_bytes=64, offset=offset)
+
+        def kept(shape, dtype, name):
+            return keep.tile(shape, dtype, name=name, align_bytes=64)
+
+        def bank(n):
+            return psum.tile([P, BANK], F32, name="bank", tag="bank%d" % n)
+
+        offs_sb = keep.tile([P, S // PER_COLUMN], U16, name="offs_sb")
+        cen_sb = keep.tile([P, V // PER_COLUMN], U16, name="cen_sb")
+        pos1_sb = keep.tile([P, V // PER_COLUMN], U16, name="pos1_sb")
+        pos2_sb = keep.tile([P, V // PER_COLUMN], U16, name="pos2_sb")
+        xs_all = placed([P, T], U8, "xs_all", AT_X_SCALES)
+        xw_all = placed([P, T], I32, "xw_all", AT_X_WORDS)
+        w1_raw = [kept([P, PACK, H // 2], F32, "w1_raw%d" % c) for c in range(2)]
+        w2s_raw = placed([P, H], U8, "w2s_raw", AT_W2_SCALES_RAW)
+        w2w_raw = placed([P, H], I32, "w2w_raw", AT_FIRST)
+        gate_sb = kept([P, 2, V], F32, "gate_sb")
 
         nc.vector.memset(xs_all[:].bitcast(I32), 0)
-        w1_rows = w1.rearrange("(p j) c -> p j c", j=PACK)
-        w2s_raw = shared.tile([P, H], U8, name="w2s_raw", align_bytes=64, offset=18304)
         nc.vector.memset(w2s_raw[:].bitcast(I32), 0)
+
+        w1_rows = w1.rearrange("(p j) c -> p j c", j=PACK)
         nc.sync.dma_start(offs_sb[:], offs)
         nc.sync.dma_start(w1_raw[0][:], w1_rows[:, :, : H // 2])
-        for q in range(4):
-            eng = nc.scalar if q < 2 else nc.sync
-            eng.dma_start(xs_all[32 * q : 32 * q + 4, :].bitcast(I32), x_scales[0, 4 * q : 4 * q + 4, :].bitcast(I32))
+        for q in range(QUADRANTS):
+            queue = nc.scalar if q < QUADRANTS // 2 else nc.sync
+            queue.dma_start(scale_rows(xs_all, q), hbm_scale_rows(x_scales, q))
         nc.sync.dma_start(pos1_sb[:], pos1)
-        nc.sync.dma_start(xw_all[:], x_words[0].rearrange("p n t -> p (n t)").bitcast(I32))
+        nc.sync.dma_start(xw_all[:], hbm_words(x_words))
         nc.sync.dma_start(w1_raw[1][:], w1_rows[:, :, H // 2 :])
         nc.sync.dma_start(pos2_sb[:], pos2)
-        for q in range(4):
-            nc.sync.dma_start(w2s_raw[32 * q : 32 * q + 4, :].bitcast(I32), w2_scales[0, 4 * q : 4 * q + 4, :].bitcast(I32))
-        w2w_raw = shared.tile([P, H], I32, name="w2w_raw", align_bytes=64, offset=14592)
-        nc.sync.dma_start(w2w_raw[:], w2_words[0].rearrange("p n t -> p (n t)").bitcast(I32))
-        gate_sb = shared.tile([P, 2, V], F32, name="gate_sb", align_bytes=64, offset=12544)
+        for q in range(QUADRANTS):
+            nc.sync.dma_start(scale_rows(w2s_raw, q), hbm_scale_rows(w2_scales, q))
+        nc.sync.dma_start(w2w_raw[:], hbm_words(w2_words))
         nc.sync.dma_start(gate_sb[:], gate.rearrange("d p v -> p d v"))
         nc.sync.dma_start(cen_sb[:], cen)
-        ident = keep.tile([P, P], F32, name="ident", align_bytes=64)
+        ident = kept([P, P], F32, "ident")
         make_identity(nc, ident[:])
 
-        xq_scales = keep.tile([P, S], U8, name="xq_scales", align_bytes=64)
+        xq_scales = kept([P, S], U8, "xq_scales")
         nc.vector.tensor_copy(xq_scales[:], xs_all[:].indirect(offs_sb[:]))
 
-        w1_words = keep.tile([P, H], U32, name="w1_words", align_bytes=64)
-        w1_scales = keep.tile([P, H], U8, name="w1_scales", align_bytes=64)
-        xq_words = shared.tile([P, S], U32, name="xq_words", align_bytes=64, offset=0)
-        for c in range(2):
-            if c == 1:
-                for g in range(2):
-                    nc.vector.tensor_copy(xq_words[:, 256 * g : 256 * (g + 1)], xw_all[:].bitcast(U32).indirect(offs_sb[:, 16 * g : 16 * (g + 1)]))
-            split = (40, 34)[c]
-            w1_bf = keep.tile([P, PACK, P // 2, PACK], BF16, name="w1_bf%d" % c, align_bytes=64)
-            src = w1_raw[c][:].rearrange("p j (m t) -> p m t j", t=PACK)
-            dst = w1_bf[:].rearrange("p t m j -> p m t j")
-            nc.vector.tensor_copy(dst[:, :split], src[:, :split])
-            nc.scalar.copy(dst[:, split:], src[:, split:])
-            for t in range(PACK):
-                cols = slice(P * t + 64 * c, P * t + 64 * (c + 1))
-                nc.vector.quantize_mx(
-                    out=w1_words[:, cols].bitcast(FP8X4), scales=w1_scales[:, cols], in_=w1_bf[:, t].rearrange("p m j -> p (m j)")
-                )
+        w1_words = kept([P, H], U32, "w1_words")
+        w1_scales = kept([P, H], U8, "w1_scales")
+        groups = H // 2 // PACK
 
-        turn_raw = shared.tile([P, PACK], F32, name="turn_raw", align_bytes=64, offset=7168)
+        def quantise_w1_half(c):
+            src = w1_raw[c][:].rearrange("p j (m t) -> p m t j", t=PACK)
+            for lo, hi, on_vector in CAST_STEPS[c]:
+                w1_bf = kept([P, hi - lo, groups, PACK], BF16, "w1_bf%d_%d" % (c, lo))
+                dst = w1_bf[:].rearrange("p t m j -> p m t j")
+                nc.vector.tensor_copy(dst[:, :on_vector], src[:, :on_vector, lo:hi])
+                nc.scalar.copy(dst[:, on_vector:], src[:, on_vector:, lo:hi])
+                for t in range(lo, hi):
+                    cols = slice(P * t + groups * c, P * t + groups * (c + 1))
+                    nc.vector.quantize_mx(
+                        out=w1_words[:, cols].bitcast(FP8X4), scales=w1_scales[:, cols], in_=w1_bf[:, t - lo].rearrange("p m j -> p (m j)")
+                    )
+
+        quantise_w1_half(0)
+        xq_words = placed([P, S], U32, "xq_words", AT_X_SCALES)
+        for g in range(2):
+            entries = slice(S // 2 * g, S // 2 * (g + 1))
+            columns = slice(entries.start // PER_COLUMN, entries.stop // PER_COLUMN)
+            nc.vector.tensor_copy(xq_words[:, entries], xw_all[:].bitcast(U32).indirect(offs_sb[:, columns]))
+        quantise_w1_half(1)
+
+        turn_raw = placed([P, PACK], F32, "turn_raw", AT_TURN)
         nc.sync.dma_start(turn_raw[:], turn.rearrange("(p t) o -> p (t o)", t=PACK))
 
-        h = [keep.tile([P, S], F32, name="h%d" % t, align_bytes=64) for t in range(PACK)]
-        pieces = [(0, 0, 256), (0, 256, 512)] + [(t, 0, S) for t in range(1, PACK)]
+        h = [kept([P, S], F32, "h%d" % t) for t in range(PACK)]
+        pieces = [(0, lo, lo + P) for lo in range(0, S, P)] + [(t, 0, S) for t in range(1, PACK)]
         for n, (t, lo, hi) in enumerate(pieces):
             rows = slice(P * t, P * (t + 1))
-            bank = psum.tile([P, 512], F32, name="bank", tag="bank%d" % n)
+            acc = bank(n)
             nc.tensor.matmul_mx(
-                out=bank[:, : hi - lo], lhsT=w1_words[:, rows].bitcast(FP8X4), lhsT_scale=w1_scales[:, rows],
+                out=acc[:, : hi - lo], lhsT=w1_words[:, rows].bitcast(FP8X4), lhsT_scale=w1_scales[:, rows],
                 rhs=xq_words[:, lo:hi].bitcast(FP8X4), rhs_scale=xq_scales[:, lo:hi], start=True, stop=True,
             )
-            nc.scalar.activation(h[t][:, lo:hi], bank[:, : hi - lo], COPY, scale=0.06)
+            nc.scalar.activation(h[t][:, lo:hi], acc[:, : hi - lo], COPY, scale=KEEP_Z * CENTRE)
 
-        w2w = shared.tile([P, H], U32, name="w2w", align_bytes=64, offset=4096)
+        w2w = placed([P, H], U32, "w2w", AT_W2_WORDS)
         nc.vector.tensor_copy(
             w2w[:].rearrange("p (t a b) -> p a t b", t=PACK, b=4),
             w2w_raw[:].bitcast(U32).rearrange("p (a b t) -> p a t b", t=PACK, b=4),
         )
-        w2s = shared.tile([P, H], U8, name="w2s", align_bytes=64, offset=6144)
+        w2s = placed([P, H], U8, "w2s", AT_W2_SCALES)
         nc.vector.tensor_copy(
             w2s[:].rearrange("p (t a b) -> p a t b", t=PACK, b=16),
             w2s_raw[:].rearrange("p (a b t) -> p a t b", t=PACK, b=16),
         )
 
-        gate9 = shared.tile([P, 2, V], F32, name="gate9", align_bytes=64, offset=0)
-        nc.scalar.activation(gate9[:], gate_sb[:], COPY, scale=9.0)
+        gate_scaled = placed([P, 2, V], F32, "gate_scaled", AT_X_SCALES)
+        nc.scalar.activation(gate_scaled[:], gate_sb[:], COPY, scale=NEIGHBOURS / CENTRE)
 
-        first = shared.tile([P, PACK, V], F32, name="first", align_bytes=64, offset=14592)
-        second = shared.tile([P, PACK, V], F32, name="second", align_bytes=64, offset=18688)
+        first = placed([P, PACK, V], F32, "first", AT_FIRST)
+        second = placed([P, PACK, V], F32, "second", AT_SECOND)
         halves = [slice(HALF * a, HALF * (a + 1)) for a in range(2)]
-        lists = [slice(HALF // 16 * a, HALF // 16 * (a + 1)) for a in range(2)]
         last = PACK - 1
-        both = [
-            [
-                shared.tile([P, HALF], F32, name="both%d_0" % t, align_bytes=64, offset=8192 + 512 * t)[:],
-                shared.tile([P, HALF], F32, name="both%d_1" % t, align_bytes=64, offset=10240 + 512 * t)[:],
-            ]
-            for t in range(last)
-        ]
-        both3 = keep.tile([P, V], F32, name="both3", align_bytes=64)
-        both.append([both3[:, c] for c in halves])
+        sums = [[placed([P, HALF], F32, "sum%d_%d" % (t, a), AT_SUMS[a] + HALF_PLANE * t)[:] for a in range(2)] for t in range(last)]
+        last_sum = kept([P, V], F32, "last_sum")
+        sums.append([last_sum[:, cols] for cols in halves])
         for t in range(PACK):
-            gates = gate9 if t == last else gate_sb
+            gates = gate_scaled if t == last else gate_sb
             nc.vector.tensor_tensor(first[:, t, :], h[t][:].indirect(pos1_sb[:]), gates[:, 0, :], MULT)
             nc.vector.tensor_tensor(second[:, t, :], h[t][:].indirect(pos2_sb[:]), gates[:, 1, :], MULT)
             if t < last:
-                turn_banks = [psum.tile([P, 512], F32, name="bank", tag="bank%d" % ((2 * t + a + 6) % 8)) for a in range(2)]
-                turned = [shared.tile([P, P], F32, name="turned%d_%d" % (t, a), align_bytes=64, offset=23040 + 512 * (2 * t + a)) for a in range(2)]
+                via = [bank((len(pieces) + 2 * t + a) % BANKS) for a in range(2)]
+                turned = [placed([P, P], F32, "turned%d_%d" % (t, a), AT_TURNED + HALF_PLANE * (2 * t + a)) for a in range(2)]
                 for a in range(2):
-                    nc.tensor.matmul(turn_banks[a][:, :P], first[:, t, halves[a]], ident[:], start=True, stop=False, is_transpose=True)
-                    nc.tensor.matmul(turn_banks[a][:, :P], second[:, t, halves[a]], ident[:], start=False, stop=True, is_transpose=True)
-                    nc.scalar.copy(turned[a][:], turn_banks[a][:, :P])
+                    nc.tensor.matmul(via[a][:, :P], first[:, t, halves[a]], ident[:], start=True, stop=False, is_transpose=True)
+                    nc.tensor.matmul(via[a][:, :P], second[:, t, halves[a]], ident[:], start=False, stop=True, is_transpose=True)
+                    nc.scalar.copy(turned[a][:], via[a][:, :P])
                 for a in range(2):
-                    nc.tensor.transpose(turn_banks[a][:, P : 2 * P], turned[a][:], ident[:])
-                    nc.scalar.activation(both[t][a], turn_banks[a][:, P : 2 * P], COPY, scale=9.0)
-        turn_sc = shared.tile([P, PACK], F32, name="turn_sc", align_bytes=64, offset=23040 + 512 * 5)
-        nc.scalar.activation(turn_sc[:], turn_raw[:], COPY, scale=0.4)
+                    nc.tensor.transpose(via[a][:, P : 2 * P], turned[a][:], ident[:])
+                    nc.scalar.activation(sums[t][a], via[a][:, P : 2 * P], COPY, scale=NEIGHBOURS / CENTRE)
+        turn_scaled = placed([P, PACK], F32, "turn_scaled", AT_TURNED + HALF_PLANE * (2 * last - 1))
+        nc.scalar.activation(turn_scaled[:], turn_raw[:], COPY, scale=MIX_Y)
 
-        o_words = keep.tile([P, V], I32, name="o_words", align_bytes=64)
-        o_scales = keep.tile([P, V], U8, name="o_scales", align_bytes=64)
-        out_rows = out_0.rearrange("(p t) v -> p t v", t=PACK)
-        out_words = out_1[0].rearrange("p n t -> p (n t)").bitcast(I32)
-        zs = [
-            keep.tile([P, PACK, HALF], F32, name="zs0", align_bytes=64),
-            shared.tile([P, PACK, HALF], F32, name="zs1", align_bytes=64, offset=8192),
-        ]
+        o_words = kept([P, V], I32, "o_words")
+        o_scales = kept([P, V], U8, "o_scales")
+        z_kept = [kept([P, PACK, HALF], F32, "z_kept0"), placed([P, PACK, HALF], F32, "z_kept1", AT_SUMS[0])]
+
+        def add_centre(a, t):
+            columns = slice(halves[a].start // PER_COLUMN, halves[a].stop // PER_COLUMN)
+            nc.vector.tensor_tensor(z_kept[a][:, t, :], h[t][:].indirect(cen_sb[:, columns]), sums[t][a], ADD)
+
+        add_centre(0, 0)
+        nc.vector.tensor_tensor(last_sum[:], first[:, last, :], second[:, last, :], ADD)
+        for t in (1, 3, 2):
+            add_centre(0, t)
+        for t in range(PACK):
+            add_centre(1, t)
+
+        z_words = [placed([P, HALF], U32, "z_words0", AT_SUMS[1] + HALF_PLANE), kept([P, HALF], U32, "z_words1")]
+        y = {}
         for a in range(2):
-            for t in ((0, 1, 3, 2), (0, 1, 2, 3))[a]:
-                nc.vector.tensor_tensor(zs[a][:, t, :], h[t][:].indirect(cen_sb[:, lists[a]]), both[t][a], ADD)
-                if (a, t) == (0, 0):
-                    nc.vector.tensor_tensor(both3[:], first[:, last, :], second[:, last, :], ADD)
-        banks = {}
-        for a in range(2):
-            z_bf = keep.tile([P, HALF, PACK], BF16, name="z_bf%d" % a, align_bytes=64)
-            woven = z_bf[:].rearrange("p (c i) t -> p c t i", i=4)
-            planes = zs[a][:].rearrange("p t (c i) -> p c t i", i=4)
+            z_bf = kept([P, HALF, PACK], BF16, "z_bf%d" % a)
+            woven, planes = weave_views(z_bf, z_kept[a])
             if a == 0:
-                nc.scalar.activation(woven, planes, COPY, scale=1.0 / 0.6)
+                nc.scalar.activation(woven, planes, COPY, scale=1.0 / KEEP_Z)
             else:
-                nc.vector.tensor_scalar_mul(woven[:, :20], planes[:, :20], 1.0 / 0.6)
-                nc.scalar.activation(woven[:, 20:], planes[:, 20:], COPY, scale=1.0 / 0.6)
-            z_words = shared.tile([P, HALF], U32, name="z_words%d" % a, align_bytes=64, offset=10752 + 1024 * a)
-            z_scales = keep.tile([P, HALF], U8, name="z_scales%d" % a, align_bytes=64)
-            nc.vector.quantize_mx(out=z_words[:].bitcast(FP8X4), scales=z_scales[:], in_=z_bf[:].rearrange("p c t -> p (c t)"))
+                nc.vector.tensor_scalar_mul(woven[:, :WEAVE_ON_VECTOR], planes[:, :WEAVE_ON_VECTOR], 1.0 / KEEP_Z)
+                nc.scalar.activation(woven[:, WEAVE_ON_VECTOR:], planes[:, WEAVE_ON_VECTOR:], COPY, scale=1.0 / KEEP_Z)
+            z_scales = kept([P, HALF], U8, "z_scales%d" % a)
+            nc.vector.quantize_mx(out=z_words[a][:].bitcast(FP8X4), scales=z_scales[:], in_=z_bf[:].rearrange("p c t -> p (c t)"))
             for t in range(PACK):
                 rows = slice(P * t, P * (t + 1))
-                banks[a, t] = psum.tile([P, 512], F32, name="bank", tag="bank%d" % (PACK * (1 - a) + t))
+                y[a, t] = bank(PACK * (1 - a) + t)[:, :HALF]
                 nc.tensor.matmul_mx(
-                    out=banks[a, t][:, :HALF], lhsT=w2w[:, rows].bitcast(FP8X4), lhsT_scale=w2s[:, rows],
-                    rhs=z_words[:].bitcast(FP8X4), rhs_scale=z_scales[:], start=True, stop=True,
+                    out=y[a, t], lhsT=w2w[:, rows].bitcast(FP8X4), lhsT_scale=w2s[:, rows],
+                    rhs=z_words[a][:].bitcast(FP8X4), rhs_scale=z_scales[:], start=True, stop=True,
                 )
+
+        out_rows = out_0.rearrange("(p t) v -> p t v", t=PACK)
         for a in range(2):
-            cols = slice(HALF * a, HALF * (a + 1))
-            res = keep.tile([P, PACK, HALF], F32, name="res%d" % a, align_bytes=64)
+            res = kept([P, PACK, HALF], F32, "res%d" % a)
             for t in range(PACK):
-                nc.vector.scalar_tensor_tensor(res[:, t, :], banks[a, t][:, :HALF], turn_sc[:, t : t + 1], zs[a][:, t, :], MULT, ADD)
-            nc.sync.dma_start(out_rows[:, :, cols], res[:])
-            res_bf = keep.tile([P, HALF, PACK], BF16, name="res_bf%d" % a, align_bytes=64)
-            woven = res_bf[:].rearrange("p (c i) t -> p c t i", i=4)
-            planes = res[:].rearrange("p t (c i) -> p c t i", i=4)
+                nc.vector.scalar_tensor_tensor(res[:, t, :], y[a, t], turn_scaled[:, t : t + 1], z_kept[a][:, t, :], MULT, ADD)
+            nc.sync.dma_start(out_rows[:, :, halves[a]], res[:])
+            res_bf = kept([P, HALF, PACK], BF16, "res_bf%d" % a)
+            woven, planes = weave_views(res_bf, res)
             if a == 0:
                 nc.scalar.copy(woven, planes)
             else:
                 nc.vector.tensor_copy(woven, planes)
             nc.vector.quantize_mx(
-                out=o_words[:, cols].bitcast(FP8X4), scales=o_scales[:, cols], in_=res_bf[:].rearrange("p c t -> p (c t)")
+                out=o_words[:, halves[a]].bitcast(FP8X4), scales=o_scales[:, halves[a]], in_=res_bf[:].rearrange("p c t -> p (c t)")
             )
-            nc.sync.dma_start(out_words[:, cols], o_words[:, cols])
-        for q in range(4):
-            eng = nc.sync if q % 2 == 0 else nc.scalar
-            eng.dma_start(out_2[0, 4 * q : 4 * q + 4, :].bitcast(I32), o_scales[32 * q : 32 * q + 4, :].bitcast(I32))
+            nc.sync.dma_start(hbm_words(out_1)[:, halves[a]], o_words[:, halves[a]])
+        for q in range(QUADRANTS):
+            queue = nc.sync if q % 2 == 0 else nc.scalar
+            queue.dma_start(hbm_scale_rows(out_2, q), scale_rows(o_scales, q))

@@ -16,20 +16,19 @@ FLOPS = 2 * K * H * S + 2 * H * H * V
 KEEP_Z, MIX_Y = 0.6, 0.4
 NEIGHBOURS, CENTRE = 0.9, 0.1
 
-CAST_STEPS = (((0, 4, 40),), ((0, 2, 32), (2, 4, 40)))
+CAST_STEPS = (((0, 4, 16),), ((0, 2, 32), (2, 4, 40)))
 WEAVE_ON_VECTOR = 20
 
 AT_X_SCALES = 0
 AT_X_WORDS = 2048
 AT_W2_WORDS = 4096
 AT_W2_SCALES = 6144
-AT_TURN = 7168
-AT_SUMS = (8192, 10240)
+AT_TURN = 6656
 AT_FIRST = 14592
 AT_SECOND = AT_FIRST + 4 * PACK * V
 AT_W2_SCALES_RAW = AT_SECOND - 384
 AT_TURNED = 23040
-HALF_PLANE = 4 * HALF
+TURNED_BYTES = 4 * P
 
 F32 = mybir.dt.float32
 BF16 = mybir.dt.bfloat16
@@ -169,7 +168,7 @@ def tile_picked_zgcnii_none_po_kernel(
         second = placed([P, PACK, V], F32, "second", AT_SECOND)
         halves = [slice(HALF * a, HALF * (a + 1)) for a in range(2)]
         last = PACK - 1
-        sums = [[placed([P, HALF], F32, "sum%d_%d" % (t, a), AT_SUMS[a] + HALF_PLANE * t)[:] for a in range(2)] for t in range(last)]
+        sums = [[kept([P, HALF], F32, "sum%d_%d" % (t, a))[:] for a in range(2)] for t in range(last)]
         last_sum = kept([P, V], F32, "last_sum")
         sums.append([last_sum[:, cols] for cols in halves])
         for t in range(PACK):
@@ -178,7 +177,7 @@ def tile_picked_zgcnii_none_po_kernel(
             nc.vector.tensor_tensor(second[:, t, :], h[t][:].indirect(pos2_sb[:]), gates[:, 1, :], MULT)
             if t < last:
                 via = [bank((len(pieces) + 2 * t + a) % BANKS) for a in range(2)]
-                turned = [placed([P, P], F32, "turned%d_%d" % (t, a), AT_TURNED + HALF_PLANE * (2 * t + a)) for a in range(2)]
+                turned = [placed([P, P], F32, "turned%d_%d" % (t, a), AT_TURNED + TURNED_BYTES * (2 * t + a)) for a in range(2)]
                 for a in range(2):
                     nc.tensor.matmul(via[a][:, :P], first[:, t, halves[a]], ident[:], start=True, stop=False, is_transpose=True)
                     nc.tensor.matmul(via[a][:, :P], second[:, t, halves[a]], ident[:], start=False, stop=True, is_transpose=True)
@@ -186,12 +185,12 @@ def tile_picked_zgcnii_none_po_kernel(
                 for a in range(2):
                     nc.tensor.transpose(via[a][:, P : 2 * P], turned[a][:], ident[:])
                     nc.scalar.activation(sums[t][a], via[a][:, P : 2 * P], COPY, scale=NEIGHBOURS / CENTRE)
-        turn_scaled = placed([P, PACK], F32, "turn_scaled", AT_TURNED + HALF_PLANE * (2 * last - 1))
+        turn_scaled = placed([P, PACK], F32, "turn_scaled", AT_TURNED + TURNED_BYTES * (2 * last - 1))
         nc.scalar.activation(turn_scaled[:], turn_raw[:], COPY, scale=MIX_Y)
 
         o_words = kept([P, V], I32, "o_words")
         o_scales = kept([P, V], U8, "o_scales")
-        z_kept = [kept([P, PACK, HALF], F32, "z_kept0"), placed([P, PACK, HALF], F32, "z_kept1", AT_SUMS[0])]
+        z_kept = [kept([P, PACK, HALF], F32, "z_kept0"), placed([P, PACK, HALF], F32, "z_kept1", AT_TURN)]
 
         def add_centre(a, t):
             columns = slice(halves[a].start // PER_COLUMN, halves[a].stop // PER_COLUMN)
@@ -204,7 +203,7 @@ def tile_picked_zgcnii_none_po_kernel(
         for t in range(PACK):
             add_centre(1, t)
 
-        z_words = [placed([P, HALF], U32, "z_words0", AT_SUMS[1] + HALF_PLANE), kept([P, HALF], U32, "z_words1")]
+        z_words = [kept([P, HALF], U32, "z_words%d" % a) for a in range(2)]
         y = {}
         for a in range(2):
             z_bf = kept([P, HALF, PACK], BF16, "z_bf%d" % a)
@@ -234,11 +233,16 @@ def tile_picked_zgcnii_none_po_kernel(
             woven, planes = weave_views(res_bf, res)
             if a == 0:
                 nc.scalar.copy(woven, planes)
+                runs = [slice(0, HALF)]
             else:
-                nc.vector.tensor_copy(woven, planes)
-            nc.vector.quantize_mx(
-                out=o_words[:, halves[a]].bitcast(FP8X4), scales=o_scales[:, halves[a]], in_=res_bf[:].rearrange("p c t -> p (c t)")
-            )
+                runs = [slice(0, HALF // 2), slice(HALF // 2, HALF)]
+                for run in runs:
+                    nc.vector.tensor_copy(woven[:, run.start // 4 : run.stop // 4], planes[:, run.start // 4 : run.stop // 4])
+            for run in runs:
+                cols = slice(halves[a].start + run.start, halves[a].start + run.stop)
+                nc.vector.quantize_mx(
+                    out=o_words[:, cols].bitcast(FP8X4), scales=o_scales[:, cols], in_=res_bf[:, run].rearrange("p c t -> p (c t)")
+                )
             nc.sync.dma_start(hbm_words(out_1)[:, halves[a]], o_words[:, halves[a]])
         for q in range(QUADRANTS):
             queue = nc.sync if q % 2 == 0 else nc.scalar

@@ -11,6 +11,7 @@ HALF = V // 2
 PER_COLUMN = 16
 BANK = 512
 BANKS = 8
+TURNED = 2
 FLOPS = 2 * K * H * S + 2 * H * H * V
 
 KEEP_Z, MIX_Y = 0.6, 0.4
@@ -55,7 +56,7 @@ def hbm_words(words):
 
 
 def weave_views(woven, planes):
-    return woven[:].rearrange("p (c i) t -> p c t i", i=4), planes[:].rearrange("p t (c i) -> p c t i", i=4)
+    return woven[:].rearrange("p (c i) t -> p c t i", i=4), planes.rearrange("p t (c i) -> p c t i", i=4)
 
 
 def tile_picked_zgcnii_none_po_kernel(
@@ -96,15 +97,14 @@ def tile_picked_zgcnii_none_po_kernel(
         for q in range(QUADRANTS):
             queue = nc.scalar if q < QUADRANTS // 2 else nc.sync
             queue.dma_start(scale_rows(xs_all, q), hbm_scale_rows(x_scales, q))
-        nc.sync.dma_start(pos1_sb[:], pos1)
+        nc.sync.dma_start(cen_sb[:], cen)
         nc.sync.dma_start(xw_all[:], hbm_words(x_words))
         nc.sync.dma_start(w1_raw[1][:], w1_rows[:, :, H // 2 :])
+        nc.sync.dma_start(pos1_sb[:], pos1)
         nc.sync.dma_start(pos2_sb[:], pos2)
-        for q in range(QUADRANTS):
-            nc.sync.dma_start(scale_rows(w2s_raw, q), hbm_scale_rows(w2_scales, q))
+        nc.sync.dma_start(w2s_raw[: 4 * QUADRANTS, :].bitcast(I32), w2_scales[0].bitcast(I32))
         nc.sync.dma_start(w2w_raw[:], hbm_words(w2_words))
         nc.sync.dma_start(gate_sb[:], gate.rearrange("d p v -> p d v"))
-        nc.sync.dma_start(cen_sb[:], cen)
         ident = kept([P, P], F32, "ident")
         make_identity(nc, ident[:])
 
@@ -140,6 +140,7 @@ def tile_picked_zgcnii_none_po_kernel(
         nc.sync.dma_start(turn_raw[:], turn.rearrange("(p t) o -> p (t o)", t=PACK))
 
         h = [kept([P, S], F32, "h%d" % t) for t in range(PACK)]
+        h_psum = {}
         pieces = [(0, lo, lo + P) for lo in range(0, S, P)] + [(t, 0, S) for t in range(1, PACK)]
         for n, (t, lo, hi) in enumerate(pieces):
             rows = slice(P * t, P * (t + 1))
@@ -148,7 +149,9 @@ def tile_picked_zgcnii_none_po_kernel(
                 out=acc[:, : hi - lo], lhsT=w1_words[:, rows].bitcast(FP8X4), lhsT_scale=w1_scales[:, rows],
                 rhs=xq_words[:, lo:hi].bitcast(FP8X4), rhs_scale=xq_scales[:, lo:hi], start=True, stop=True,
             )
-            nc.scalar.activation(h[t][:, lo:hi], acc[:, : hi - lo], COPY, scale=KEEP_Z * CENTRE)
+            if t == 0:
+                nc.scalar.activation(h[t][:, lo:hi], acc[:, : hi - lo], COPY, scale=KEEP_Z * NEIGHBOURS)
+            h_psum[t] = acc
 
         w2w = placed([P, H], U32, "w2w", AT_W2_WORDS)
         nc.vector.tensor_copy(
@@ -161,58 +164,76 @@ def tile_picked_zgcnii_none_po_kernel(
             w2s_raw[:].rearrange("p (a b t) -> p a t b", t=PACK, b=16),
         )
 
-        gate_scaled = placed([P, 2, V], F32, "gate_scaled", AT_X_SCALES)
-        nc.scalar.activation(gate_scaled[:], gate_sb[:], COPY, scale=NEIGHBOURS / CENTRE)
+        for q in range(1, QUADRANTS):
+            nc.sync.dma_start(scale_rows(w2s, q), w2s[4 * q : 4 * q + 4, :].bitcast(I32))
 
         first = placed([P, PACK, V], F32, "first", AT_FIRST)
         second = placed([P, PACK, V], F32, "second", AT_SECOND)
+        centre_first = placed([P, V], F32, "centre_first", AT_TURNED)
+        centre_rest = placed([P, PACK - 1, V], F32, "centre_rest", AT_TURNED)
+        centre = [centre_first[:]] + [centre_rest[:, t, :] for t in range(PACK - 1)]
+        z_kept = kept([P, PACK, V], F32, "z_kept")
         halves = [slice(HALF * a, HALF * (a + 1)) for a in range(2)]
-        last = PACK - 1
-        sums = [[kept([P, HALF], F32, "sum%d_%d" % (t, a))[:] for a in range(2)] for t in range(last)]
-        last_sum = kept([P, V], F32, "last_sum")
-        sums.append([last_sum[:, cols] for cols in halves])
-        for t in range(PACK):
-            gates = gate_scaled if t == last else gate_sb
-            nc.vector.tensor_tensor(first[:, t, :], h[t][:].indirect(pos1_sb[:]), gates[:, 0, :], MULT)
-            nc.vector.tensor_tensor(second[:, t, :], h[t][:].indirect(pos2_sb[:]), gates[:, 1, :], MULT)
-            if t < last:
-                via = [bank((len(pieces) + 2 * t + a) % BANKS) for a in range(2)]
-                turned = [placed([P, P], F32, "turned%d_%d" % (t, a), AT_TURNED + TURNED_BYTES * (2 * t + a)) for a in range(2)]
-                for a in range(2):
-                    nc.tensor.matmul(via[a][:, :P], first[:, t, halves[a]], ident[:], start=True, stop=False, is_transpose=True)
-                    nc.tensor.matmul(via[a][:, :P], second[:, t, halves[a]], ident[:], start=False, stop=True, is_transpose=True)
-                    nc.scalar.copy(turned[a][:], via[a][:, :P])
-                for a in range(2):
-                    nc.tensor.transpose(via[a][:, P : 2 * P], turned[a][:], ident[:])
-                    nc.scalar.activation(sums[t][a], via[a][:, P : 2 * P], COPY, scale=NEIGHBOURS / CENTRE)
-        turn_scaled = placed([P, PACK], F32, "turn_scaled", AT_TURNED + TURNED_BYTES * (2 * last - 1))
-        nc.scalar.activation(turn_scaled[:], turn_raw[:], COPY, scale=MIX_Y)
+        via = [bank(t) for t in range(TURNED)]
+        turned = [kept([P, V], F32, "turned%d" % t) for t in range(TURNED)]
 
+        def leave_psum(t):
+            nc.scalar.activation(h[t][:], h_psum[t][:], COPY, scale=KEEP_Z * NEIGHBOURS)
+
+        def gather_centre(t):
+            nc.scalar.activation(centre[t], h[t][:].indirect(cen_sb[:]), COPY, scale=CENTRE / NEIGHBOURS)
+
+        def gather(t):
+            nc.vector.tensor_tensor(first[:, t, :], h[t][:].indirect(pos1_sb[:]), gate_sb[:, 0, :], MULT)
+            nc.vector.tensor_tensor(second[:, t, :], h[t][:].indirect(pos2_sb[:]), gate_sb[:, 1, :], MULT)
+
+        def sum_turned(t):
+            terms = [centre[t], first[:, t, :], second[:, t, :]]
+            for a, cols in enumerate(halves):
+                for n, term in enumerate(terms[a:] + terms[:a]):
+                    nc.tensor.matmul(via[t][:, cols], term[:, cols], ident[:], start=n == 0, stop=n == 2, is_transpose=True)
+
+        def turn_back(t):
+            nc.scalar.copy(turned[t][:], via[t][:, :V])
+            for cols in halves:
+                nc.tensor.transpose(via[t][:, V + cols.start : V + cols.stop], turned[t][:, cols], ident[:])
+
+        def keep_z(t):
+            nc.scalar.copy(z_kept[:, t, :], via[t][:, V:])
+
+        leave_psum(1)
+        gather_centre(0)
+        gather(0)
+        sum_turned(0)
+        leave_psum(2)
+        leave_psum(3)
+        for t in range(1, PACK):
+            gather(t)
+        turn_back(0)
+        gather_centre(1)
+        sum_turned(1)
+        gather_centre(2)
+        keep_z(0)
+        gather_centre(3)
+        turn_back(1)
+        keep_z(1)
+        turn_scaled = kept([P, PACK], F32, "turn_scaled")
+        nc.scalar.activation(turn_scaled[:], turn_raw[:], COPY, scale=MIX_Y)
+        part = kept([P, PACK - TURNED, V], F32, "part")
+        for cols in halves:
+            nc.vector.tensor_tensor(part[:, :, cols], first[:, TURNED:, cols], second[:, TURNED:, cols], ADD)
+        for cols in halves:
+            nc.vector.tensor_tensor(z_kept[:, TURNED:, cols], part[:, :, cols], centre_rest[:, TURNED - 1 :, cols], ADD)
         o_words = kept([P, V], I32, "o_words")
         o_scales = kept([P, V], U8, "o_scales")
-        z_kept = [kept([P, PACK, HALF], F32, "z_kept0"), placed([P, PACK, HALF], F32, "z_kept1", AT_TURN)]
-
-        def add_centre(a, t):
-            columns = slice(halves[a].start // PER_COLUMN, halves[a].stop // PER_COLUMN)
-            nc.vector.tensor_tensor(z_kept[a][:, t, :], h[t][:].indirect(cen_sb[:, columns]), sums[t][a], ADD)
-
-        add_centre(0, 0)
-        nc.vector.tensor_tensor(last_sum[:], first[:, last, :], second[:, last, :], ADD)
-        for t in (1, 3, 2):
-            add_centre(0, t)
-        for t in range(PACK):
-            add_centre(1, t)
 
         z_words = [kept([P, HALF], U32, "z_words%d" % a) for a in range(2)]
         y = {}
         for a in range(2):
             z_bf = kept([P, HALF, PACK], BF16, "z_bf%d" % a)
-            woven, planes = weave_views(z_bf, z_kept[a])
-            if a == 0:
-                nc.scalar.activation(woven, planes, COPY, scale=1.0 / KEEP_Z)
-            else:
-                nc.vector.tensor_scalar_mul(woven[:, :WEAVE_ON_VECTOR], planes[:, :WEAVE_ON_VECTOR], 1.0 / KEEP_Z)
-                nc.scalar.activation(woven[:, WEAVE_ON_VECTOR:], planes[:, WEAVE_ON_VECTOR:], COPY, scale=1.0 / KEEP_Z)
+            woven, planes = weave_views(z_bf, z_kept[:, :, halves[a]])
+            nc.vector.tensor_scalar_mul(woven[:, :WEAVE_ON_VECTOR], planes[:, :WEAVE_ON_VECTOR], 1.0 / KEEP_Z)
+            nc.scalar.activation(woven[:, WEAVE_ON_VECTOR:], planes[:, WEAVE_ON_VECTOR:], COPY, scale=1.0 / KEEP_Z)
             z_scales = kept([P, HALF], U8, "z_scales%d" % a)
             nc.vector.quantize_mx(out=z_words[a][:].bitcast(FP8X4), scales=z_scales[:], in_=z_bf[:].rearrange("p c t -> p (c t)"))
             for t in range(PACK):
@@ -227,10 +248,10 @@ def tile_picked_zgcnii_none_po_kernel(
         for a in range(2):
             res = kept([P, PACK, HALF], F32, "res%d" % a)
             for t in range(PACK):
-                nc.vector.scalar_tensor_tensor(res[:, t, :], y[a, t], turn_scaled[:, t : t + 1], z_kept[a][:, t, :], MULT, ADD)
+                nc.vector.scalar_tensor_tensor(res[:, t, :], y[a, t], turn_scaled[:, t : t + 1], z_kept[:, t, halves[a]], MULT, ADD)
             nc.sync.dma_start(out_rows[:, :, halves[a]], res[:])
             res_bf = kept([P, HALF, PACK], BF16, "res_bf%d" % a)
-            woven, planes = weave_views(res_bf, res)
+            woven, planes = weave_views(res_bf, res[:])
             if a == 0:
                 nc.scalar.copy(woven, planes)
                 runs = [slice(0, HALF)]

@@ -11,7 +11,9 @@ HALF = V // 2
 PER_COLUMN = 16
 BANK = 512
 BANKS = 8
-TURNED = 2
+SUM_BANKS = ((0, 1), (2, 3), (7, 4))
+BACK_BANKS = ((5,), (6,), (0, 1))
+TURNED = 3
 FLOPS = 2 * K * H * S + 2 * H * H * V
 
 KEEP_Z, MIX_Y = 0.6, 0.4
@@ -169,61 +171,61 @@ def tile_picked_zgcnii_none_po_kernel(
 
         first = placed([P, PACK, V], F32, "first", AT_FIRST)
         second = placed([P, PACK, V], F32, "second", AT_SECOND)
-        centre_first = placed([P, V], F32, "centre_first", AT_TURNED)
-        centre_rest = placed([P, PACK - 1, V], F32, "centre_rest", AT_TURNED)
-        centre = [centre_first[:]] + [centre_rest[:, t, :] for t in range(PACK - 1)]
+        centre = [placed([P, V], F32, "centre%d" % t, AT_TURNED + 4 * V * (t % TURNED)) for t in range(PACK)]
         z_kept = kept([P, PACK, V], F32, "z_kept")
         halves = [slice(HALF * a, HALF * (a + 1)) for a in range(2)]
-        via = [bank(t) for t in range(TURNED)]
         turned = [kept([P, V], F32, "turned%d" % t) for t in range(TURNED)]
+        via, back = {}, {}
 
         def leave_psum(t):
             nc.scalar.activation(h[t][:], h_psum[t][:], COPY, scale=KEEP_Z * NEIGHBOURS)
 
         def gather_centre(t):
-            nc.scalar.activation(centre[t], h[t][:].indirect(cen_sb[:]), COPY, scale=CENTRE / NEIGHBOURS)
+            nc.scalar.activation(centre[t][:], h[t][:].indirect(cen_sb[:]), COPY, scale=CENTRE / NEIGHBOURS)
 
         def gather(t):
             nc.vector.tensor_tensor(first[:, t, :], h[t][:].indirect(pos1_sb[:]), gate_sb[:, 0, :], MULT)
             nc.vector.tensor_tensor(second[:, t, :], h[t][:].indirect(pos2_sb[:]), gate_sb[:, 1, :], MULT)
 
-        def sum_turned(t):
-            terms = [centre[t], first[:, t, :], second[:, t, :]]
-            for a, cols in enumerate(halves):
-                for n, term in enumerate(terms[a:] + terms[:a]):
-                    nc.tensor.matmul(via[t][:, cols], term[:, cols], ident[:], start=n == 0, stop=n == 2, is_transpose=True)
+        def sum_turned(t, terms):
+            via[t] = [bank(n) for n in SUM_BANKS[t]]
+            for n, term in enumerate(terms):
+                for a, cols in enumerate(halves):
+                    nc.tensor.matmul(via[t][a][:, :P], term[:, cols], ident[:], start=n == 0, stop=n == 2, is_transpose=True)
 
         def turn_back(t):
-            nc.scalar.copy(turned[t][:], via[t][:, :V])
-            for cols in halves:
-                nc.tensor.transpose(via[t][:, V + cols.start : V + cols.stop], turned[t][:, cols], ident[:])
+            back[t] = [bank(n) for n in BACK_BANKS[t]]
+            for a, cols in enumerate(halves):
+                nc.scalar.copy(turned[t][:, cols], via[t][a][:, :P])
+                nc.tensor.transpose(back[t][a % len(back[t])][:, cols], turned[t][:, cols], ident[:])
 
         def keep_z(t):
-            nc.scalar.copy(z_kept[:, t, :], via[t][:, V:])
+            if len(back[t]) == 1:
+                nc.scalar.copy(z_kept[:, t, :], back[t][0][:, :V])
+            else:
+                for a, cols in enumerate(halves):
+                    nc.scalar.copy(z_kept[:, t, cols], back[t][a][:, cols])
 
-        leave_psum(1)
-        gather_centre(0)
-        gather(0)
-        sum_turned(0)
-        leave_psum(2)
-        leave_psum(3)
         for t in range(1, PACK):
+            leave_psum(t)
+        for t in range(PACK):
             gather(t)
-        turn_back(0)
-        gather_centre(1)
-        sum_turned(1)
-        gather_centre(2)
-        keep_z(0)
-        gather_centre(3)
-        turn_back(1)
-        keep_z(1)
+        for t in range(TURNED):
+            gather_centre(t)
+            terms = [first[:, t, :], second[:, t, :]]
+            terms.insert(2 if t == 0 else 1, centre[t][:])
+            sum_turned(t, terms)
+        for t in range(TURNED - 1):
+            turn_back(t)
+        gather_centre(TURNED)
+        turn_back(TURNED - 1)
+        for t in range(TURNED):
+            keep_z(t)
         turn_scaled = kept([P, PACK], F32, "turn_scaled")
         nc.scalar.activation(turn_scaled[:], turn_raw[:], COPY, scale=MIX_Y)
-        part = kept([P, PACK - TURNED, V], F32, "part")
-        for cols in halves:
-            nc.vector.tensor_tensor(part[:, :, cols], first[:, TURNED:, cols], second[:, TURNED:, cols], ADD)
-        for cols in halves:
-            nc.vector.tensor_tensor(z_kept[:, TURNED:, cols], part[:, :, cols], centre_rest[:, TURNED - 1 :, cols], ADD)
+        part = kept([P, V], F32, "part")
+        nc.vector.tensor_tensor(part[:], first[:, TURNED, :], centre[TURNED][:], ADD)
+        nc.vector.tensor_tensor(z_kept[:, TURNED, :], part[:], second[:, TURNED, :], ADD)
         o_words = kept([P, V], I32, "o_words")
         o_scales = kept([P, V], U8, "o_scales")
 

@@ -7,31 +7,16 @@ K, T, S, V, H = 512, 2048, 512, 256, 512
 P = 128
 PACK = 4
 QUADRANTS = 4
+TILES = H // P
 HALF = V // 2
 PER_COLUMN = 16
 BANK = 512
-BANKS = 8
-SUM_BANKS = ((0, 1), (2, 3), (7, 4))
-BACK_BANKS = ((5,), (6,), (0, 1))
-TURNED = 3
 FLOPS = 2 * K * H * S + 2 * H * H * V
 
 KEEP_Z, MIX_Y = 0.6, 0.4
 NEIGHBOURS, CENTRE = 0.9, 0.1
 
-CAST_STEPS = (((0, 4, 16),), ((0, 2, 32), (2, 4, 40)))
 WEAVE_ON_VECTOR = 20
-
-AT_X_SCALES = 0
-AT_X_WORDS = 2048
-AT_W2_WORDS = 4096
-AT_W2_SCALES = 6144
-AT_TURN = 6656
-AT_FIRST = 14592
-AT_SECOND = AT_FIRST + 4 * PACK * V
-AT_W2_SCALES_RAW = AT_SECOND - 384
-AT_TURNED = 23040
-TURNED_BYTES = 4 * P
 
 F32 = mybir.dt.float32
 BF16 = mybir.dt.bfloat16
@@ -58,7 +43,11 @@ def hbm_words(words):
 
 
 def weave_views(woven, planes):
-    return woven[:].rearrange("p (c i) t -> p c t i", i=4), planes.rearrange("p t (c i) -> p c t i", i=4)
+    return woven.rearrange("p (c i) t -> p c t i", i=4), planes.rearrange("p t (c i) -> p c t i", i=4)
+
+
+def list_columns(offsets, entries):
+    return offsets[:, entries.start // PER_COLUMN : entries.stop // PER_COLUMN]
 
 
 def tile_picked_zgcnii_none_po_kernel(
@@ -79,16 +68,18 @@ def tile_picked_zgcnii_none_po_kernel(
         def bank(n):
             return psum.tile([P, BANK], F32, name="bank", tag="bank%d" % n)
 
+
         offs_sb = keep.tile([P, S // PER_COLUMN], U16, name="offs_sb")
         cen_sb = keep.tile([P, V // PER_COLUMN], U16, name="cen_sb")
         pos1_sb = keep.tile([P, V // PER_COLUMN], U16, name="pos1_sb")
         pos2_sb = keep.tile([P, V // PER_COLUMN], U16, name="pos2_sb")
-        xs_all = placed([P, T], U8, "xs_all", AT_X_SCALES)
-        xw_all = placed([P, T], I32, "xw_all", AT_X_WORDS)
+        xs_all = kept([P, T], U8, "xs_all")
+        xw_all = kept([P, T], I32, "xw_all")
         w1_raw = [kept([P, PACK, H // 2], F32, "w1_raw%d" % c) for c in range(2)]
-        w2s_raw = placed([P, H], U8, "w2s_raw", AT_W2_SCALES_RAW)
-        w2w_raw = placed([P, H], I32, "w2w_raw", AT_FIRST)
+        w2s_raw = kept([P, H], U8, "w2s_raw")
+        w2w_raw = kept([P, H], I32, "w2w_raw")
         gate_sb = kept([P, 2, V], F32, "gate_sb")
+        turn_raw = kept([P, PACK], F32, "turn_raw")
 
         nc.vector.memset(xs_all[:].bitcast(I32), 0)
         nc.vector.memset(w2s_raw[:].bitcast(I32), 0)
@@ -104,146 +95,172 @@ def tile_picked_zgcnii_none_po_kernel(
         nc.sync.dma_start(w1_raw[1][:], w1_rows[:, :, H // 2 :])
         nc.sync.dma_start(pos1_sb[:], pos1)
         nc.sync.dma_start(pos2_sb[:], pos2)
-        nc.sync.dma_start(w2s_raw[: 4 * QUADRANTS, :].bitcast(I32), w2_scales[0].bitcast(I32))
-        nc.sync.dma_start(w2w_raw[:], hbm_words(w2_words))
         nc.sync.dma_start(gate_sb[:], gate.rearrange("d p v -> p d v"))
+        nc.sync.dma_start(w2w_raw[:], hbm_words(w2_words))
+        for q in range(QUADRANTS):
+            nc.sync.dma_start(scale_rows(w2s_raw, q), hbm_scale_rows(w2_scales, q))
+        nc.sync.dma_start(turn_raw[:], turn.rearrange("(p t) o -> p (t o)", t=PACK))
         ident = kept([P, P], F32, "ident")
         make_identity(nc, ident[:])
 
         xq_scales = kept([P, S], U8, "xq_scales")
         nc.vector.tensor_copy(xq_scales[:], xs_all[:].indirect(offs_sb[:]))
 
-        w1_words = kept([P, H], U32, "w1_words")
-        w1_scales = kept([P, H], U8, "w1_scales")
         groups = H // 2 // PACK
+        w1_words = [kept([P, P], U32, "w1_words%d" % c) for c in range(TILES)]
+        w1_scales = [kept([P, P], U8, "w1_scales%d" % c) for c in range(TILES)]
+        w1_bf = {}
 
-        def quantise_w1_half(c):
+        def cast(c, lo, hi, on_vector):
             src = w1_raw[c][:].rearrange("p j (m t) -> p m t j", t=PACK)
-            for lo, hi, on_vector in CAST_STEPS[c]:
-                w1_bf = kept([P, hi - lo, groups, PACK], BF16, "w1_bf%d_%d" % (c, lo))
-                dst = w1_bf[:].rearrange("p t m j -> p m t j")
+            woven = kept([P, hi - lo, groups, PACK], BF16, "w1_bf%d_%d" % (c, lo))
+            dst = woven[:].rearrange("p t m j -> p m t j")
+            if on_vector > 0:
                 nc.vector.tensor_copy(dst[:, :on_vector], src[:, :on_vector, lo:hi])
+            if on_vector < groups:
                 nc.scalar.copy(dst[:, on_vector:], src[:, on_vector:, lo:hi])
-                for t in range(lo, hi):
-                    cols = slice(P * t + groups * c, P * t + groups * (c + 1))
-                    nc.vector.quantize_mx(
-                        out=w1_words[:, cols].bitcast(FP8X4), scales=w1_scales[:, cols], in_=w1_bf[:, t - lo].rearrange("p m j -> p (m j)")
-                    )
+            for t in range(lo, hi):
+                w1_bf[c, t] = (woven, t - lo)
 
-        quantise_w1_half(0)
-        xq_words = placed([P, S], U32, "xq_words", AT_X_SCALES)
-        for g in range(2):
-            entries = slice(S // 2 * g, S // 2 * (g + 1))
-            columns = slice(entries.start // PER_COLUMN, entries.stop // PER_COLUMN)
-            nc.vector.tensor_copy(xq_words[:, entries], xw_all[:].bitcast(U32).indirect(offs_sb[:, columns]))
-        quantise_w1_half(1)
+        def quantise_pair(c):
+            woven, at = w1_bf[c, 0]
+            nc.vector.quantize_mx(
+                out=w1_words[c][:].bitcast(FP8X4), scales=w1_scales[c][:], in_=woven[:, at : at + 2].rearrange("p t m j -> p (t m j)")
+            )
 
-        turn_raw = placed([P, PACK], F32, "turn_raw", AT_TURN)
-        nc.sync.dma_start(turn_raw[:], turn.rearrange("(p t) o -> p (t o)", t=PACK))
+        def quantise_plane(c, t):
+            woven, at = w1_bf[c, t]
+            cols = slice(groups * c, groups * (c + 1))
+            nc.vector.quantize_mx(
+                out=w1_words[t][:, cols].bitcast(FP8X4), scales=w1_scales[t][:, cols], in_=woven[:, at].rearrange("p m j -> p (m j)")
+            )
 
-        h = [kept([P, S], F32, "h%d" % t) for t in range(PACK)]
+        h = [kept([P, S], F32, "h0"), kept([P, S], F32, "h1"), placed([P, S], F32, "h2", 0), kept([P, S], F32, "h3")]
         h_psum = {}
-        pieces = [(0, lo, lo + P) for lo in range(0, S, P)] + [(t, 0, S) for t in range(1, PACK)]
-        for n, (t, lo, hi) in enumerate(pieces):
-            rows = slice(P * t, P * (t + 1))
+        first = [kept([P, V], F32, "first%d" % c) for c in range(TILES)]
+        second = [kept([P, V], F32, "second%d" % c) for c in range(TILES)]
+        centre = [kept([P, V], F32, "centre%d" % c) for c in range(TILES)]
+        halves = [slice(HALF * a, HALF * (a + 1)) for a in range(2)]
+        turned = [kept([P, 3, P], F32, "turned%d" % a) for a in range(2)]
+        z_kept = kept([P, PACK, V], F32, "z_kept")
+        sums, back = {}, {}
+
+        def multiply(c, cols, n):
             acc = bank(n)
             nc.tensor.matmul_mx(
-                out=acc[:, : hi - lo], lhsT=w1_words[:, rows].bitcast(FP8X4), lhsT_scale=w1_scales[:, rows],
-                rhs=xq_words[:, lo:hi].bitcast(FP8X4), rhs_scale=xq_scales[:, lo:hi], start=True, stop=True,
+                out=acc[:, : cols.stop - cols.start], lhsT=w1_words[c][:].bitcast(FP8X4), lhsT_scale=w1_scales[c][:],
+                rhs=xq_words[:, cols].bitcast(FP8X4), rhs_scale=xq_scales[:, cols], start=True, stop=True,
             )
-            if t == 0:
-                nc.scalar.activation(h[t][:, lo:hi], acc[:, : hi - lo], COPY, scale=KEEP_Z * NEIGHBOURS)
-            h_psum[t] = acc
+            h_psum[c, cols.start] = acc
 
-        w2w = placed([P, H], U32, "w2w", AT_W2_WORDS)
+        def leave_psum(c, cols):
+            nc.scalar.activation(h[c][:, cols], h_psum[c, cols.start][:, : cols.stop - cols.start], COPY, scale=KEEP_Z * NEIGHBOURS)
+
+        def gather_first(c):
+            nc.vector.tensor_tensor(first[c][:], h[c][:].indirect(pos1_sb[:]), gate_sb[:, 0, :], MULT)
+
+        def gather_second(c):
+            nc.vector.tensor_tensor(second[c][:], h[c][:].indirect(pos2_sb[:]), gate_sb[:, 1, :], MULT)
+
+        def gather_centre(c):
+            nc.scalar.activation(centre[c][:], h[c][:].indirect(cen_sb[:]), COPY, scale=CENTRE / NEIGHBOURS)
+
+        def sum_turned(c, a, acc, at):
+            for n, term in enumerate((first[c], centre[c], second[c])):
+                nc.tensor.matmul(acc[:, at : at + P], term[:, halves[a]], ident[:], start=n == 0, stop=n == 2, is_transpose=True)
+
+        cast(0, 0, 4, 16)
+        quantise_pair(0)
+        quantise_plane(0, 2)
+        quantise_plane(0, 3)
+        xq_words = kept([P, S], U32, "xq_words")
+        pieces = [slice(0, 256), slice(256, 384), slice(384, 512)]
+        for n, cols in enumerate(pieces):
+            nc.vector.tensor_copy(xq_words[:, cols], xw_all[:].bitcast(U32).indirect(list_columns(offs_sb, cols)))
+            multiply(0, cols, n)
+            leave_psum(0, cols)
+        everything = slice(0, S)
+        cast(1, 0, 2, 64)
+        cast(1, 2, 4, 64)
+        quantise_pair(1)
+        multiply(1, everything, 3)
+        gather_first(0)
+        gather_centre(0)
+        leave_psum(1, everything)
+        quantise_plane(1, 2)
+        quantise_plane(1, 3)
+        multiply(2, everything, 0)
+        multiply(3, everything, 1)
+        gather_second(0)
+        leave_psum(2, everything)
+        for a in range(2):
+            sums[a] = bank(4 + a)
+            sum_turned(0, a, sums[a], 0)
+        gather_first(1)
+        gather_second(1)
+        gather_centre(1)
+        leave_psum(3, everything)
+        for a in range(2):
+            sum_turned(1, a, sums[a], P)
+        gather_first(2)
+        gather_second(2)
+        gather_centre(2)
+        for a in range(2):
+            nc.scalar.copy(
+                turned[a][:, 0:2, :].rearrange("v t (c m) -> v c t m", c=2), sums[a][:, : 2 * P].rearrange("v (c t m) -> v c t m", c=2, t=2)
+            )
+        for a in range(2):
+            sums[2, a] = bank(6 + a)
+            sum_turned(2, a, sums[2, a], 0)
+        for t in range(2):
+            back[t] = bank(2 + t)
+            for a in range(2):
+                nc.tensor.transpose(back[t][:, halves[a]], turned[a][:, t, :], ident[:])
+        gather_first(3)
+        gather_second(3)
+        for a in range(2):
+            nc.scalar.copy(turned[a][:, 2, :], sums[2, a][:, :P])
+            back[2, a] = bank(a)
+            nc.tensor.transpose(back[2, a][:, :P], turned[a][:, 2, :], ident[:])
+        gather_centre(3)
+        for t in range(2):
+            nc.scalar.copy(z_kept[:, t, :], back[t][:, :V])
+        for a in range(2):
+            nc.scalar.copy(z_kept[:, 2, halves[a]], back[2, a][:, :P])
+        turn_scaled = kept([P, PACK], F32, "turn_scaled")
+        nc.scalar.activation(turn_scaled[:], turn_raw[:], COPY, scale=MIX_Y)
+
+        part = kept([P, V], F32, "part")
+        nc.vector.tensor_tensor(part[:], first[3][:], centre[3][:], ADD)
+        w2w = placed([P, H], U32, "w2w", 0)
         nc.vector.tensor_copy(
             w2w[:].rearrange("p (t a b) -> p a t b", t=PACK, b=4),
             w2w_raw[:].bitcast(U32).rearrange("p (a b t) -> p a t b", t=PACK, b=4),
         )
-        w2s = placed([P, H], U8, "w2s", AT_W2_SCALES)
+        nc.vector.tensor_tensor(z_kept[:, 3, :], part[:], second[3][:], ADD)
+        w2s = kept([P, H], U8, "w2s")
         nc.vector.tensor_copy(
             w2s[:].rearrange("p (t a b) -> p a t b", t=PACK, b=16),
             w2s_raw[:].rearrange("p (a b t) -> p a t b", t=PACK, b=16),
         )
 
-        for q in range(1, QUADRANTS):
-            nc.sync.dma_start(scale_rows(w2s, q), w2s[4 * q : 4 * q + 4, :].bitcast(I32))
-
-        first = placed([P, PACK, V], F32, "first", AT_FIRST)
-        second = placed([P, PACK, V], F32, "second", AT_SECOND)
-        centre = [placed([P, V], F32, "centre%d" % t, AT_TURNED + 4 * V * (t % TURNED)) for t in range(PACK)]
-        z_kept = kept([P, PACK, V], F32, "z_kept")
-        halves = [slice(HALF * a, HALF * (a + 1)) for a in range(2)]
-        turned = [kept([P, V], F32, "turned%d" % t) for t in range(TURNED)]
-        via, back = {}, {}
-
-        def leave_psum(t):
-            nc.scalar.activation(h[t][:], h_psum[t][:], COPY, scale=KEEP_Z * NEIGHBOURS)
-
-        def gather_centre(t):
-            nc.scalar.activation(centre[t][:], h[t][:].indirect(cen_sb[:]), COPY, scale=CENTRE / NEIGHBOURS)
-
-        def gather(t):
-            nc.vector.tensor_tensor(first[:, t, :], h[t][:].indirect(pos1_sb[:]), gate_sb[:, 0, :], MULT)
-            nc.vector.tensor_tensor(second[:, t, :], h[t][:].indirect(pos2_sb[:]), gate_sb[:, 1, :], MULT)
-
-        def sum_turned(t, terms):
-            via[t] = [bank(n) for n in SUM_BANKS[t]]
-            for n, term in enumerate(terms):
-                for a, cols in enumerate(halves):
-                    nc.tensor.matmul(via[t][a][:, :P], term[:, cols], ident[:], start=n == 0, stop=n == 2, is_transpose=True)
-
-        def turn_back(t):
-            back[t] = [bank(n) for n in BACK_BANKS[t]]
-            for a, cols in enumerate(halves):
-                nc.scalar.copy(turned[t][:, cols], via[t][a][:, :P])
-                nc.tensor.transpose(back[t][a % len(back[t])][:, cols], turned[t][:, cols], ident[:])
-
-        def keep_z(t):
-            if len(back[t]) == 1:
-                nc.scalar.copy(z_kept[:, t, :], back[t][0][:, :V])
-            else:
-                for a, cols in enumerate(halves):
-                    nc.scalar.copy(z_kept[:, t, cols], back[t][a][:, cols])
-
-        for t in range(1, PACK):
-            leave_psum(t)
-        for t in range(PACK):
-            gather(t)
-        for t in range(TURNED):
-            gather_centre(t)
-            terms = [first[:, t, :], second[:, t, :]]
-            terms.insert(2 if t == 0 else 1, centre[t][:])
-            sum_turned(t, terms)
-        for t in range(TURNED - 1):
-            turn_back(t)
-        gather_centre(TURNED)
-        turn_back(TURNED - 1)
-        for t in range(TURNED):
-            keep_z(t)
-        turn_scaled = kept([P, PACK], F32, "turn_scaled")
-        nc.scalar.activation(turn_scaled[:], turn_raw[:], COPY, scale=MIX_Y)
-        part = kept([P, V], F32, "part")
-        nc.vector.tensor_tensor(part[:], first[:, TURNED, :], centre[TURNED][:], ADD)
-        nc.vector.tensor_tensor(z_kept[:, TURNED, :], part[:], second[:, TURNED, :], ADD)
         o_words = kept([P, V], I32, "o_words")
         o_scales = kept([P, V], U8, "o_scales")
-
-        z_words = [kept([P, HALF], U32, "z_words%d" % a) for a in range(2)]
         y = {}
         for a in range(2):
             z_bf = kept([P, HALF, PACK], BF16, "z_bf%d" % a)
-            woven, planes = weave_views(z_bf, z_kept[:, :, halves[a]])
+            woven, planes = weave_views(z_bf[:], z_kept[:, :, halves[a]])
             nc.vector.tensor_scalar_mul(woven[:, :WEAVE_ON_VECTOR], planes[:, :WEAVE_ON_VECTOR], 1.0 / KEEP_Z)
             nc.scalar.activation(woven[:, WEAVE_ON_VECTOR:], planes[:, WEAVE_ON_VECTOR:], COPY, scale=1.0 / KEEP_Z)
+            z_words = kept([P, HALF], U32, "z_words%d" % a)
             z_scales = kept([P, HALF], U8, "z_scales%d" % a)
-            nc.vector.quantize_mx(out=z_words[a][:].bitcast(FP8X4), scales=z_scales[:], in_=z_bf[:].rearrange("p c t -> p (c t)"))
+            nc.vector.quantize_mx(out=z_words[:].bitcast(FP8X4), scales=z_scales[:], in_=z_bf[:].rearrange("p c t -> p (c t)"))
             for t in range(PACK):
                 rows = slice(P * t, P * (t + 1))
-                y[a, t] = bank(PACK * (1 - a) + t)[:, :HALF]
+                y[a, t] = bank((PACK * (1 - a) + t))[:, :HALF]
                 nc.tensor.matmul_mx(
                     out=y[a, t], lhsT=w2w[:, rows].bitcast(FP8X4), lhsT_scale=w2s[:, rows],
-                    rhs=z_words[a][:].bitcast(FP8X4), rhs_scale=z_scales[:], start=True, stop=True,
+                    rhs=z_words[:].bitcast(FP8X4), rhs_scale=z_scales[:], start=True, stop=True,
                 )
 
         out_rows = out_0.rearrange("(p t) v -> p t v", t=PACK)
@@ -253,7 +270,7 @@ def tile_picked_zgcnii_none_po_kernel(
                 nc.vector.scalar_tensor_tensor(res[:, t, :], y[a, t], turn_scaled[:, t : t + 1], z_kept[:, t, halves[a]], MULT, ADD)
             nc.sync.dma_start(out_rows[:, :, halves[a]], res[:])
             res_bf = kept([P, HALF, PACK], BF16, "res_bf%d" % a)
-            woven, planes = weave_views(res_bf, res[:])
+            woven, planes = weave_views(res_bf[:], res[:])
             if a == 0:
                 nc.scalar.copy(woven, planes)
                 runs = [slice(0, HALF)]

@@ -85,8 +85,8 @@ def tile_picked_zgcnii_none_po_kernel(
         nc.vector.memset(w2s_raw[:].bitcast(I32), 0)
 
         w1_rows = w1.rearrange("(p j) c -> p j c", j=PACK)
-        nc.sync.dma_start(offs_sb[:], offs)
         nc.sync.dma_start(w1_raw[0][:], w1_rows[:, :, : H // 2])
+        nc.sync.dma_start(offs_sb[:], offs)
         for q in range(QUADRANTS):
             queue = nc.scalar if q < QUADRANTS // 2 else nc.sync
             queue.dma_start(scale_rows(xs_all, q), hbm_scale_rows(x_scales, q))

@@ -93,9 +93,9 @@ def tile_picked_zgcnii_none_po_kernel(
         nc.sync.dma_start(cen_sb[:], cen)
         nc.sync.dma_start(xw_all[:], hbm_words(x_words))
         nc.sync.dma_start(w1_raw[1][:], w1_rows[:, :, H // 2 :])
+        nc.sync.dma_start(gate_sb[:], gate.rearrange("d p v -> p d v"))
         nc.sync.dma_start(pos1_sb[:], pos1)
         nc.sync.dma_start(pos2_sb[:], pos2)
-        nc.sync.dma_start(gate_sb[:], gate.rearrange("d p v -> p d v"))
         nc.sync.dma_start(w2w_raw[:], hbm_words(w2_words))
         for q in range(QUADRANTS):
             nc.sync.dma_start(scale_rows(w2s_raw, q), hbm_scale_rows(w2_scales, q))
@@ -135,7 +135,7 @@ def tile_picked_zgcnii_none_po_kernel(
                 out=w1_words[t][:, cols].bitcast(FP8X4), scales=w1_scales[t][:, cols], in_=woven[:, at].rearrange("p m j -> p (m j)")
             )
 
-        h = [kept([P, S], F32, "h0"), kept([P, S], F32, "h1"), placed([P, S], F32, "h2", 0), kept([P, S], F32, "h3")]
+        h = [kept([P, S], F32, "h0"), kept([P, S], F32, "h1"), kept([P, S], F32, "h2"), placed([P, S], F32, "h3", 0)]
         h_psum = {}
         first = [kept([P, V], F32, "first%d" % c) for c in range(TILES)]
         second = [kept([P, V], F32, "second%d" % c) for c in range(TILES)]
@@ -184,11 +184,11 @@ def tile_picked_zgcnii_none_po_kernel(
         cast(1, 2, 4, 64)
         quantise_pair(1)
         multiply(1, everything, 3)
+        quantise_plane(1, 2)
+        quantise_plane(1, 3)
         gather_first(0)
         gather_centre(0)
         leave_psum(1, everything)
-        quantise_plane(1, 2)
-        quantise_plane(1, 3)
         multiply(2, everything, 0)
         multiply(3, everything, 1)
         gather_second(0)

@@ -17,6 +17,7 @@ KEEP_Z, MIX_Y = 0.6, 0.4
 NEIGHBOURS, CENTRE = 0.9, 0.1
 
 WEAVE_ON_VECTOR = 20
+LATE_CAST_ON_VECTOR = 64
 
 F32 = mybir.dt.float32
 BF16 = mybir.dt.bfloat16
@@ -107,8 +108,13 @@ def tile_picked_zgcnii_none_po_kernel(
         nc.vector.tensor_copy(xq_scales[:], xs_all[:].indirect(offs_sb[:]))
 
         groups = H // 2 // PACK
-        w1_words = [kept([P, P], U32, "w1_words%d" % c) for c in range(TILES)]
-        w1_scales = [kept([P, P], U8, "w1_scales%d" % c) for c in range(TILES)]
+        w1_words = [kept([P, P], U32, "w1_words%d" % c)[:] for c in range(2)]
+        w1_scales = [kept([P, P], U8, "w1_scales%d" % c)[:] for c in range(2)]
+        late_words = kept([P, 2 * P], U32, "late_words")
+        late_scales = kept([P, 2 * P], U8, "late_scales")
+        for cols in (slice(P, 2 * P), slice(0, P)):
+            w1_words.append(late_words[:, cols])
+            w1_scales.append(late_scales[:, cols])
         w1_bf = {}
 
         def cast(c, lo, hi, on_vector):
@@ -125,14 +131,14 @@ def tile_picked_zgcnii_none_po_kernel(
         def quantise_pair(c):
             woven, at = w1_bf[c, 0]
             nc.vector.quantize_mx(
-                out=w1_words[c][:].bitcast(FP8X4), scales=w1_scales[c][:], in_=woven[:, at : at + 2].rearrange("p t m j -> p (t m j)")
+                out=w1_words[c].bitcast(FP8X4), scales=w1_scales[c], in_=woven[:, at : at + 2].rearrange("p t m j -> p (t m j)")
             )
 
-        def quantise_plane(c, t):
+        def quantise_late(c, t, count, at_col):
             woven, at = w1_bf[c, t]
-            cols = slice(groups * c, groups * (c + 1))
+            cols = slice(at_col, at_col + groups * count)
             nc.vector.quantize_mx(
-                out=w1_words[t][:, cols].bitcast(FP8X4), scales=w1_scales[t][:, cols], in_=woven[:, at].rearrange("p m j -> p (m j)")
+                out=late_words[:, cols].bitcast(FP8X4), scales=late_scales[:, cols], in_=woven[:, at : at + count].rearrange("p t m j -> p (t m j)")
             )
 
         h = [kept([P, S], F32, "h0"), kept([P, S], F32, "h1"), kept([P, S], F32, "h2"), placed([P, S], F32, "h3", 0)]
@@ -148,7 +154,7 @@ def tile_picked_zgcnii_none_po_kernel(
         def multiply(c, cols, n):
             acc = bank(n)
             nc.tensor.matmul_mx(
-                out=acc[:, : cols.stop - cols.start], lhsT=w1_words[c][:].bitcast(FP8X4), lhsT_scale=w1_scales[c][:],
+                out=acc[:, : cols.stop - cols.start], lhsT=w1_words[c].bitcast(FP8X4), lhsT_scale=w1_scales[c],
                 rhs=xq_words[:, cols].bitcast(FP8X4), rhs_scale=xq_scales[:, cols], start=True, stop=True,
             )
             h_psum[c, cols.start] = acc
@@ -171,8 +177,8 @@ def tile_picked_zgcnii_none_po_kernel(
 
         cast(0, 0, 4, 16)
         quantise_pair(0)
-        quantise_plane(0, 2)
-        quantise_plane(0, 3)
+        quantise_late(0, 2, 1, 0)
+        quantise_late(0, 3, 1, 3 * groups)
         xq_words = kept([P, S], U32, "xq_words")
         pieces = [slice(0, 256), slice(256, 384), slice(384, 512)]
         for n, cols in enumerate(pieces):
@@ -181,11 +187,10 @@ def tile_picked_zgcnii_none_po_kernel(
             leave_psum(0, cols)
         everything = slice(0, S)
         cast(1, 0, 2, 64)
-        cast(1, 2, 4, 64)
+        cast(1, 2, 4, LATE_CAST_ON_VECTOR)
         quantise_pair(1)
         multiply(1, everything, 3)
-        quantise_plane(1, 2)
-        quantise_plane(1, 3)
+        quantise_late(1, 2, 2, groups)
         gather_first(0)
         gather_centre(0)
         leave_psum(1, everything)
@@ -219,14 +224,16 @@ def tile_picked_zgcnii_none_po_kernel(
         gather_first(3)
         gather_second(3)
         for a in range(2):
-            nc.scalar.copy(turned[a][:, 2, :], sums[2, a][:, :P])
+            nc.scalar.copy(
+                turned[a][:, 2, :].rearrange("v (c m) -> v c m", c=2), sums[2, a][:, :P].rearrange("v (c m) -> v c m", c=2)[:, ::-1, :]
+            )
             back[2, a] = bank(a)
             nc.tensor.transpose(back[2, a][:, :P], turned[a][:, 2, :], ident[:])
         gather_centre(3)
         for t in range(2):
             nc.scalar.copy(z_kept[:, t, :], back[t][:, :V])
         for a in range(2):
-            nc.scalar.copy(z_kept[:, 2, halves[a]], back[2, a][:, :P])
+            nc.scalar.copy(z_kept[:, 3, halves[a]], back[2, a][:, :P])
         turn_scaled = kept([P, PACK], F32, "turn_scaled")
         nc.scalar.activation(turn_scaled[:], turn_raw[:], COPY, scale=MIX_Y)
 
@@ -237,7 +244,7 @@ def tile_picked_zgcnii_none_po_kernel(
             w2w[:].rearrange("p (t a b) -> p a t b", t=PACK, b=4),
             w2w_raw[:].bitcast(U32).rearrange("p (a b t) -> p a t b", t=PACK, b=4),
         )
-        nc.vector.tensor_tensor(z_kept[:, 3, :], part[:], second[3][:], ADD)
+        nc.vector.tensor_tensor(z_kept[:, 2, :], part[:], second[3][:], ADD)
         w2s = kept([P, H], U8, "w2s")
         nc.vector.tensor_copy(
             w2s[:].rearrange("p (t a b) -> p a t b", t=PACK, b=16),
@@ -268,7 +275,10 @@ def tile_picked_zgcnii_none_po_kernel(
             res = kept([P, PACK, HALF], F32, "res%d" % a)
             for t in range(PACK):
                 nc.vector.scalar_tensor_tensor(res[:, t, :], y[a, t], turn_scaled[:, t : t + 1], z_kept[:, t, halves[a]], MULT, ADD)
-            nc.sync.dma_start(out_rows[:, :, halves[a]], res[:])
+                if a == 1 and t % 2 == 1:
+                    nc.sync.dma_start(out_rows[:, t - 1 : t + 1, halves[a]], res[:, t - 1 : t + 1, :])
+            if a == 0:
+                nc.sync.dma_start(out_rows[:, :, halves[a]], res[:])
             res_bf = kept([P, HALF, PACK], BF16, "res_bf%d" % a)
             woven, planes = weave_views(res_bf[:], res[:])
             if a == 0:
@@ -283,7 +293,7 @@ def tile_picked_zgcnii_none_po_kernel(
                 nc.vector.quantize_mx(
                     out=o_words[:, cols].bitcast(FP8X4), scales=o_scales[:, cols], in_=res_bf[:, run].rearrange("p c t -> p (c t)")
                 )
-            nc.sync.dma_start(hbm_words(out_1)[:, halves[a]], o_words[:, halves[a]])
+        nc.sync.dma_start(hbm_words(out_1), o_words[:])
         for q in range(QUADRANTS):
             queue = nc.sync if q % 2 == 0 else nc.scalar
             queue.dma_start(hbm_scale_rows(out_2, q), scale_rows(o_scales, q))

@@ -286,8 +286,8 @@ def tile_picked_zgcnii_none_po_kernel(
                 runs = [slice(0, HALF)]
             else:
                 runs = [slice(0, HALF // 2), slice(HALF // 2, HALF)]
-                for run in runs:
-                    nc.vector.tensor_copy(woven[:, run.start // 4 : run.stop // 4], planes[:, run.start // 4 : run.stop // 4])
+                for run, copy_on in zip(runs, (nc.vector.tensor_copy, nc.scalar.copy)):
+                    copy_on(woven[:, run.start // 4 : run.stop // 4], planes[:, run.start // 4 : run.stop // 4])
             for run in runs:
                 cols = slice(halves[a].start + run.start, halves[a].start + run.stop)
                 nc.vector.quantize_mx(

from contextlib import ExitStack

import concourse.mybir as mybir
from concourse.masks import make_identity

K, T, S, V, H = 512, 2048, 512, 256, 512
P = 128
PACK = 4
QUADRANTS = 4
TILES = H // P
HALF = V // 2
PER_COLUMN = 16
BANK = 512
FLOPS = 2 * K * H * S + 2 * H * H * V

KEEP_Z, MIX_Y = 0.6, 0.4
NEIGHBOURS, CENTRE = 0.9, 0.1

WEAVE_ON_VECTOR = 20
LATE_CAST_ON_VECTOR = 64

F32 = mybir.dt.float32
BF16 = mybir.dt.bfloat16
I32 = mybir.dt.int32
U32 = mybir.dt.uint32
U16 = mybir.dt.uint16
U8 = mybir.dt.uint8
FP8X4 = mybir.dt.float8_e4m3fn_x4
MULT = mybir.AluOpType.mult
ADD = mybir.AluOpType.add
COPY = mybir.ActivationFunctionType.Copy


def scale_rows(tile, q):
    return tile[32 * q : 32 * q + 4, :].bitcast(I32)


def hbm_scale_rows(scales, q):
    return scales[0, 4 * q : 4 * q + 4, :].bitcast(I32)


def hbm_words(words):
    return words[0].rearrange("p n r -> p (n r)").bitcast(I32)


def weave_views(woven, planes):
    return woven.rearrange("p (c i) t -> p c t i", i=4), planes.rearrange("p t (c i) -> p c t i", i=4)


def list_columns(offsets, entries):
    return offsets[:, entries.start // PER_COLUMN : entries.stop // PER_COLUMN]


def tile_picked_zgcnii_none_po_kernel(
    tc, x_words, x_scales, w1, w2_words, w2_scales, gate, turn, offs, cen, pos1, pos2, out_0, out_1, out_2
):
    nc = tc.nc
    with ExitStack() as ctx:
        keep = ctx.enter_context(tc.tile_pool(name="keep", bufs=1))
        shared = ctx.enter_context(tc.tile_pool(name="shared", bufs=1))
        psum = ctx.enter_context(tc.psum_pool(name="psum", bufs=1))

        def placed(shape, dtype, name, offset):
            return shared.tile(shape, dtype, name=name, align_bytes=64, offset=offset)

        def kept(shape, dtype, name):
            return keep.tile(shape, dtype, name=name, align_bytes=64)

        def bank(n):
            return psum.tile([P, BANK], F32, name="bank", tag="bank%d" % n)


        offs_sb = keep.tile([P, S // PER_COLUMN], U16, name="offs_sb")
        cen_sb = keep.tile([P, V // PER_COLUMN], U16, name="cen_sb")
        pos1_sb = keep.tile([P, V // PER_COLUMN], U16, name="pos1_sb")
        pos2_sb = keep.tile([P, V // PER_COLUMN], U16, name="pos2_sb")
        xs_all = kept([P, T], U8, "xs_all")
        xw_all = kept([P, T], I32, "xw_all")
        w1_raw = [kept([P, PACK, H // 2], F32, "w1_raw%d" % c) for c in range(2)]
        w2s_raw = kept([P, H], U8, "w2s_raw")
        w2w_raw = kept([P, H], I32, "w2w_raw")
        gate_sb = kept([P, 2, V], F32, "gate_sb")
        turn_raw = kept([P, PACK], F32, "turn_raw")

        nc.vector.memset(xs_all[:].bitcast(I32), 0)
        nc.vector.memset(w2s_raw[:].bitcast(I32), 0)

        w1_rows = w1.rearrange("(p j) c -> p j c", j=PACK)
        nc.sync.dma_start(w1_raw[0][:], w1_rows[:, :, : H // 2])
        nc.sync.dma_start(offs_sb[:], offs)
        for q in range(QUADRANTS):
            queue = nc.scalar if q < QUADRANTS // 2 else nc.sync
            queue.dma_start(scale_rows(xs_all, q), hbm_scale_rows(x_scales, q))
        nc.sync.dma_start(cen_sb[:], cen)
        nc.sync.dma_start(xw_all[:], hbm_words(x_words))
        nc.sync.dma_start(w1_raw[1][:], w1_rows[:, :, H // 2 :])
        nc.sync.dma_start(gate_sb[:], gate.rearrange("d p v -> p d v"))
        nc.sync.dma_start(pos1_sb[:], pos1)
        nc.sync.dma_start(pos2_sb[:], pos2)
        nc.sync.dma_start(w2w_raw[:], hbm_words(w2_words))
        for q in range(QUADRANTS):
            nc.sync.dma_start(scale_rows(w2s_raw, q), hbm_scale_rows(w2_scales, q))
        nc.sync.dma_start(turn_raw[:], turn.rearrange("(p t) o -> p (t o)", t=PACK))
        ident = kept([P, P], F32, "ident")
        make_identity(nc, ident[:])

        xq_scales = kept([P, S], U8, "xq_scales")
        nc.vector.tensor_copy(xq_scales[:], xs_all[:].indirect(offs_sb[:]))

        groups = H // 2 // PACK
        w1_words = [kept([P, P], U32, "w1_words%d" % c)[:] for c in range(2)]
        w1_scales = [kept([P, P], U8, "w1_scales%d" % c)[:] for c in range(2)]
        late_words = kept([P, 2 * P], U32, "late_words")
        late_scales = kept([P, 2 * P], U8, "late_scales")
        for cols in (slice(P, 2 * P), slice(0, P)):
            w1_words.append(late_words[:, cols])
            w1_scales.append(late_scales[:, cols])
        w1_bf = {}

        def cast(c, lo, hi, on_vector):
            src = w1_raw[c][:].rearrange("p j (m t) -> p m t j", t=PACK)
            woven = kept([P, hi - lo, groups, PACK], BF16, "w1_bf%d_%d" % (c, lo))
            dst = woven[:].rearrange("p t m j -> p m t j")
            if on_vector > 0:
                nc.vector.tensor_copy(dst[:, :on_vector], src[:, :on_vector, lo:hi])
            if on_vector < groups:
                nc.scalar.copy(dst[:, on_vector:], src[:, on_vector:, lo:hi])
            for t in range(lo, hi):
                w1_bf[c, t] = (woven, t - lo)

        def quantise_pair(c):
            woven, at = w1_bf[c, 0]
            nc.vector.quantize_mx(
                out=w1_words[c].bitcast(FP8X4), scales=w1_scales[c], in_=woven[:, at : at + 2].rearrange("p t m j -> p (t m j)")
            )

        def quantise_late(c, t, count, at_col):
            woven, at = w1_bf[c, t]
            cols = slice(at_col, at_col + groups * count)
            nc.vector.quantize_mx(
                out=late_words[:, cols].bitcast(FP8X4), scales=late_scales[:, cols], in_=woven[:, at : at + count].rearrange("p t m j -> p (t m j)")
            )

        h = [kept([P, S], F32, "h0"), kept([P, S], F32, "h1"), kept([P, S], F32, "h2"), placed([P, S], F32, "h3", 0)]
        h_psum = {}
        first = [kept([P, V], F32, "first%d" % c) for c in range(TILES)]
        second = [kept([P, V], F32, "second%d" % c) for c in range(TILES)]
        centre = [kept([P, V], F32, "centre%d" % c) for c in range(TILES)]
        halves = [slice(HALF * a, HALF * (a + 1)) for a in range(2)]
        turned = [kept([P, 3, P], F32, "turned%d" % a) for a in range(2)]
        z_kept = kept([P, PACK, V], F32, "z_kept")
        sums, back = {}, {}

        def multiply(c, cols, n):
            acc = bank(n)
            nc.tensor.matmul_mx(
                out=acc[:, : cols.stop - cols.start], lhsT=w1_words[c].bitcast(FP8X4), lhsT_scale=w1_scales[c],
                rhs=xq_words[:, cols].bitcast(FP8X4), rhs_scale=xq_scales[:, cols], start=True, stop=True,
            )
            h_psum[c, cols.start] = acc

        def leave_psum(c, cols):
            nc.scalar.activation(h[c][:, cols], h_psum[c, cols.start][:, : cols.stop - cols.start], COPY, scale=KEEP_Z * NEIGHBOURS)

        def gather_first(c):
            nc.vector.tensor_tensor(first[c][:], h[c][:].indirect(pos1_sb[:]), gate_sb[:, 0, :], MULT)

        def gather_second(c):
            nc.vector.tensor_tensor(second[c][:], h[c][:].indirect(pos2_sb[:]), gate_sb[:, 1, :], MULT)

        def gather_centre(c):
            nc.scalar.activation(centre[c][:], h[c][:].indirect(cen_sb[:]), COPY, scale=CENTRE / NEIGHBOURS)

        def sum_turned(c, a, acc, at):
            for n, term in enumerate((first[c], centre[c], second[c])):
                nc.tensor.matmul(acc[:, at : at + P], term[:, halves[a]], ident[:], start=n == 0, stop=n == 2, is_transpose=True)

        cast(0, 0, 4, 16)
        quantise_pair(0)
        quantise_late(0, 2, 1, 0)
        quantise_late(0, 3, 1, 3 * groups)
        xq_words = kept([P, S], U32, "xq_words")
        pieces = [slice(0, 256), slice(256, 384), slice(384, 512)]
        for n, cols in enumerate(pieces):
            nc.vector.tensor_copy(xq_words[:, cols], xw_all[:].bitcast(U32).indirect(list_columns(offs_sb, cols)))
            multiply(0, cols, n)
            leave_psum(0, cols)
        everything = slice(0, S)
        cast(1, 0, 2, 64)
        cast(1, 2, 4, LATE_CAST_ON_VECTOR)
        quantise_pair(1)
        multiply(1, everything, 3)
        quantise_late(1, 2, 2, groups)
        gather_first(0)
        gather_centre(0)
        leave_psum(1, everything)
        multiply(2, everything, 0)
        multiply(3, everything, 1)
        gather_second(0)
        leave_psum(2, everything)
        for a in range(2):
            sums[a] = bank(4 + a)
            sum_turned(0, a, sums[a], 0)
        gather_first(1)
        gather_second(1)
        gather_centre(1)
        leave_psum(3, everything)
        for a in range(2):
            sum_turned(1, a, sums[a], P)
        gather_first(2)
        gather_second(2)
        gather_centre(2)
        for a in range(2):
            nc.scalar.copy(
                turned[a][:, 0:2, :].rearrange("v t (c m) -> v c t m", c=2), sums[a][:, : 2 * P].rearrange("v (c t m) -> v c t m", c=2, t=2)
            )
        for a in range(2):
            sums[2, a] = bank(6 + a)
            sum_turned(2, a, sums[2, a], 0)
        for t in range(2):
            back[t] = bank(2 + t)
            for a in range(2):
                nc.tensor.transpose(back[t][:, halves[a]], turned[a][:, t, :], ident[:])
        gather_first(3)
        gather_second(3)
        for a in range(2):
            nc.scalar.copy(
                turned[a][:, 2, :].rearrange("v (c m) -> v c m", c=2), sums[2, a][:, :P].rearrange("v (c m) -> v c m", c=2)[:, ::-1, :]
            )
            back[2, a] = bank(a)
            nc.tensor.transpose(back[2, a][:, :P], turned[a][:, 2, :], ident[:])
        gather_centre(3)
        for t in range(2):
            nc.scalar.copy(z_kept[:, t, :], back[t][:, :V])
        for a in range(2):
            nc.scalar.copy(z_kept[:, 3, halves[a]], back[2, a][:, :P])
        turn_scaled = kept([P, PACK], F32, "turn_scaled")
        nc.scalar.activation(turn_scaled[:], turn_raw[:], COPY, scale=MIX_Y)

        part = kept([P, V], F32, "part")
        nc.vector.tensor_tensor(part[:], first[3][:], centre[3][:], ADD)
        w2w = placed([P, H], U32, "w2w", 0)
        nc.vector.tensor_copy(
            w2w[:].rearrange("p (t a b) -> p a t b", t=PACK, b=4),
            w2w_raw[:].bitcast(U32).rearrange("p (a b t) -> p a t b", t=PACK, b=4),
        )
        nc.vector.tensor_tensor(z_kept[:, 2, :], part[:], second[3][:], ADD)
        w2s = kept([P, H], U8, "w2s")
        nc.vector.tensor_copy(
            w2s[:].rearrange("p (t a b) -> p a t b", t=PACK, b=16),
            w2s_raw[:].rearrange("p (a b t) -> p a t b", t=PACK, b=16),
        )

        o_words = kept([P, V], I32, "o_words")
        o_scales = kept([P, V], U8, "o_scales")
        y = {}
        for a in range(2):
            z_bf = kept([P, HALF, PACK], BF16, "z_bf%d" % a)
            woven, planes = weave_views(z_bf[:], z_kept[:, :, halves[a]])
            nc.vector.tensor_scalar_mul(woven[:, :WEAVE_ON_VECTOR], planes[:, :WEAVE_ON_VECTOR], 1.0 / KEEP_Z)
            nc.scalar.activation(woven[:, WEAVE_ON_VECTOR:], planes[:, WEAVE_ON_VECTOR:], COPY, scale=1.0 / KEEP_Z)
            z_words = kept([P, HALF], U32, "z_words%d" % a)
            z_scales = kept([P, HALF], U8, "z_scales%d" % a)
            nc.vector.quantize_mx(out=z_words[:].bitcast(FP8X4), scales=z_scales[:], in_=z_bf[:].rearrange("p c t -> p (c t)"))
            for t in range(PACK):
                rows = slice(P * t, P * (t + 1))
                y[a, t] = bank((PACK * (1 - a) + t))[:, :HALF]
                nc.tensor.matmul_mx(
                    out=y[a, t], lhsT=w2w[:, rows].bitcast(FP8X4), lhsT_scale=w2s[:, rows],
                    rhs=z_words[:].bitcast(FP8X4), rhs_scale=z_scales[:], start=True, stop=True,
                )

        out_rows = out_0.rearrange("(p t) v -> p t v", t=PACK)
        for a in range(2):
            res = kept([P, PACK, HALF], F32, "res%d" % a)
            for t in range(PACK):
                nc.vector.scalar_tensor_tensor(res[:, t, :], y[a, t], turn_scaled[:, t : t + 1], z_kept[:, t, halves[a]], MULT, ADD)
                if a == 1 and t % 2 == 1:
                    nc.sync.dma_start(out_rows[:, t - 1 : t + 1, halves[a]], res[:, t - 1 : t + 1, :])
            if a == 0:
                nc.sync.dma_start(out_rows[:, :, halves[a]], res[:])
            res_bf = kept([P, HALF, PACK], BF16, "res_bf%d" % a)
            woven, planes = weave_views(res_bf[:], res[:])
            if a == 0:
                nc.scalar.copy(woven, planes)
                runs = [slice(0, HALF)]
            else:
                runs = [slice(0, HALF // 2), slice(HALF // 2, HALF)]
                for run, copy_on in zip(runs, (nc.vector.tensor_copy, nc.scalar.copy)):
                    copy_on(woven[:, run.start // 4 : run.stop // 4], planes[:, run.start // 4 : run.stop // 4])
            for run in runs:
                cols = slice(halves[a].start + run.start, halves[a].start + run.stop)
                nc.vector.quantize_mx(
                    out=o_words[:, cols].bitcast(FP8X4), scales=o_scales[:, cols], in_=res_bf[:, run].rearrange("p c t -> p (c t)")
                )
        nc.sync.dma_start(hbm_words(out_1), o_words[:])
        for q in range(QUADRANTS):
            queue = nc.sync if q % 2 == 0 else nc.scalar
            queue.dma_start(hbm_scale_rows(out_2, q), scale_rows(o_scales, q))
